import numpy as np, ml_dtypes
CORES = [40,64,80,88,96,104,120,144]
N = 8
import mx_ref
BF = ml_dtypes.bfloat16
def gentries(a):
    return np.ascontiguousarray(a.reshape(8, 16, -1).transpose(0, 2, 1)).reshape(8, -1)
def gtable(e):
    e = np.asarray(e); return np.ascontiguousarray(e.reshape(8, -1, 16).transpose(0, 2, 1)).reshape(128, -1).astype(np.int32)
def gcols(t, e):
    v = np.concatenate([t.reshape(8, 16, -1, 4), np.zeros((8, 16, 1, 4), BF)], axis=2)
    return np.ascontiguousarray(np.stack([v[g][:, e[g]] for g in range(8)])).reshape(128, -1)
def gpick(z, e):
    return np.concatenate([z[16 * g:16 * g + 16][:, e[g]] for g in range(8)])
def tile(rs):
    return np.stack(rs, axis=2).reshape(128, -1).astype(BF)
def pick(q, e):
    c = np.concatenate([q[0].reshape(128, -1, 4), np.zeros((128, 1, 4), np.uint8)], axis=1); s = np.concatenate([q[1], np.ones((16, 1), np.uint8)], axis=1)
    return (np.ascontiguousarray(c[:, e].reshape(128, -1)), np.ascontiguousarray(s[:, e]))
def join(*qs):
    return (np.concatenate([q[0] for q in qs], axis=1), np.concatenate([q[1] for q in qs], axis=1))
def put(q, e, v):
    c, s = q[0].reshape(128, -1, 4).copy(), q[1].copy(); c[:, e] = v[0].reshape(128, -1, 4); s[:, e] = v[1]
    return (c.reshape(128, -1), s)
def pk(c, s):
    return (np.ascontiguousarray(c), mx_ref.live(s))
def emit(q):
    return q[0], q[1]
def packed(v, rng):
    q = [mx_ref.quantize(np.ascontiguousarray(v[r])) for r in range(N)]
    return np.stack([a for a, b in q]), np.stack([mx_ref.plane(b, rng) for a, b in q])
def values_of_codes():
    e, c = np.zeros((128, 128, 4), np.float32), np.zeros((128, 2, 4), np.uint8)
    e[np.arange(128), np.arange(128), 0] = 1
    c[:127, :, 0] = np.arange(256).reshape(2, 128).T[:127]
    return mx_ref.matmul(mx_ref.quantize(e.reshape(128, 512).astype(BF)), (c.reshape(128, 8), np.full((16, 2), 127, np.uint8))).T.reshape(-1).astype(np.float64)
CODE_VALUE, SCALE_VALUE = values_of_codes(), 2.0 ** (np.arange(256) - 127.0)
def decode(q):
    return (CODE_VALUE[q[0]].reshape(16, 8, -1, 4) * SCALE_VALUE[q[1]][:, None, :, None] + 0.0).reshape(128, -1).astype(np.float32)
def f(rng, *shape):
    return mx_ref.flush((rng.standard_normal(shape, dtype=np.float32) * np.exp2(rng.integers(-2, 3, shape[:-1] + (1,)))).astype(BF))
def wide(rng, *shape, cols=0):
    v = rng.standard_normal(shape, dtype=np.float32) * np.exp2(rng.integers(-12, 13, shape)).astype(np.float32)
    if cols: v *= np.repeat(np.exp2(rng.integers(-cols, cols + 1, shape[:-2] + (1, shape[-1] // 4))) * (rng.random(shape[:-2] + (1, shape[-1] // 4)) > 0.0625), 4, axis=-1).astype(np.float32)
    return mx_ref.flush(v.astype(BF))
C = 288
STEP = [4, 1, 2]
def numbers_of(rng):
    return {"x": np.array(f(rng, N, 128, 4 * C)), "u": np.array(f(rng, N, 128, 512)), "v": np.array(f(rng, N, 128, 512))}
def stored(k):
    return {"od": np.stack([gtable(k[r]) for r in range(N)])}
def orders(rng):
    return stored(rng.permuted(np.tile(np.arange(C), (N, 8, 1)), axis=2))
def rings(rng):
    h = rng.permutation(8)
    pairs = [1] + [2] * (C // 2 - 1) + [1]
    sizes = [[C], [C], [1, C - 1], [257, C - 257], pairs, pairs, [C // 2, C // 2], [1] * C]
    i = np.arange(N)
    odd = (i ^ (i >> 1) ^ (i >> 2)) % 2
    k = np.zeros((N, 8, C), np.int64)
    for g in range(8):
        w = np.arange(C) if h[g] % 2 == 0 else rng.permutation(C)
        c, after = rng.permutation(C), np.zeros(C, np.int64)
        a = 0
        for m in sizes[h[g]]:
            after[w[a:a + m]] = np.roll(w[a:a + m], -1)
            a += m
        k[:, g] = np.where(odd[:, None] == 1, c[after], c)
    return stored(k)
def layers(rng):
    return np.array(f(rng, N, 128, 2048)).reshape(N, 8, 16, 4, 8, 16, 4)
def weights(rng, w):
    c, s = packed(np.ascontiguousarray(w).reshape(N, 128, 2048), rng)
    return {"wc": c, "ws": s}
def setup_inputs(rng):
    return {**numbers_of(rng), **orders(rng), **weights(rng, layers(rng))}
def setup_inputs_ties(rng):
    d = numbers_of(rng)
    o = rng.permutation(N)
    k = rng.integers(-1, 2, (N, 8, C)).astype(np.float32)
    k[o[0]] = 0
    k[o[1]] = 1
    k[o[2]] = -1
    x = d["x"].reshape(N, 8, 16, C, 4)
    x[:, :, 0] = 0
    x[:, :, 0, :, 0] = k.astype(BF)
    u = d["u"].reshape(N, 128, 128, 4)
    u[:, :, ::16] = 0
    for h in range(0, 128, 16): u[:, h, h, 0] = 1
    w = layers(rng)
    w[:, :, :, :, :, 0] = 0
    return {"x": x.reshape(N, 128, 4 * C), "u": u.reshape(N, 128, 512), "v": d["v"], **rings(rng), **weights(rng, w)}
def setup_inputs_near(rng):
    d = numbers_of(rng)
    small = ((np.arange(N) & STEP[1]) > 0) ^ (rng.random() < 0.5)
    k = np.where(small, 2.0 ** -30, 1.0)
    x = d["x"].astype(np.float32).reshape(N, 8, 16, C, 4)
    x[:, :, :8] = 0
    s = rng.integers(-1, 2, (N, 8, C)) * k[:, None, None]
    x[:, :, 0, :, 0] = 1.125 * s
    x[:, :, 1, :, 0] = -1.25 * s
    x[:, :, 2, :, 0] = rng.choice([-1.0, 1.0], (N, 8, C)) * 2.0 ** -30
    x[:, :, 4, :, 0] = 2.0 ** -30
    for r in range(N):
        at = [0, C - 1, int(rng.integers(C)), int(rng.integers(C))]
        for g, j in zip(rng.permutation(8)[:4], at): x[r, g, 0, j, 0] = 2.0 ** 30 * rng.choice([-1.0, 1.0])
    k = k.astype(np.float32)
    u = d["u"].reshape(N, 128, 128, 4)
    u[:, :, ::16] = 0
    for h in range(0, 128, 16):
        u[:, h, h, 0] = (1.125 * k).astype(BF)
        u[:, h + 1, h, 0] = k.astype(BF)
        u[:, h + 3, h, 0] = k.astype(BF)
    w = layers(rng)
    w[:, :, :8] = 0
    w[:, :, :, :, :, :8] = 0
    for r in range(N):
        for g in range(8):
            if small[r]: w[r, g, 2, 0, g, 3, 0] = 2.0 ** -8
    return {"x": x.reshape(N, 128, 4 * C).astype(BF), "u": u.reshape(N, 128, 512), "v": d["v"], **orders(rng), **weights(rng, w)}
def setup_inputs_odd(rng):
    d = numbers_of(rng)
    x = (1.0 + (2 * rng.integers(0, 64, (N, 16, 8, C, 4)) + 1) * 2.0 ** -7) * np.exp2(-rng.integers(0, 7, (N, 16, 8, C, 4)).astype(np.float64)) * rng.choice([-1.0, 1.0], (N, 16, 8, C, 4))
    x[:, :, 0, :, 0] = np.where(rng.random((N, 16, C)) < 0.5, 1.96875, 1.875) * 2.0 ** 8 * rng.choice([-1.0, 1.0], (N, 16, 1))
    x[:, ::2, 1, :, 0] = rng.integers(7, 10, (N, 8, C)) * 2.0 ** -8
    x[:, ::2, 2, :, 0] = -8 * 2.0 ** -8
    u = d["u"].reshape(N, 16, 8, 128, 4)
    u[:, :, :, ::16] = 0
    for g in range(8): u[:, 2 * g, 1:3, 16 * g, 0] = 1
    w = layers(rng)
    for i in (0, 8):
        w[:, :, i] = 0
        w[:, :, :, :, :, i] = 0
    return {"x": x.astype(np.float32).reshape(N, 128, 4 * C).astype(BF), "u": u.reshape(N, 128, 512), "v": d["v"], **orders(rng), **weights(rng, w)}
def setup_inputs_ends(rng):
    d = numbers_of(rng)
    o, most = rng.permutation(N) % 4, rng.permutation(N) % 2
    h, e = rng.permutation(8), int(rng.integers(8))
    c = np.where(h < 2, 0.0, h % 2 * 2.0 - 1.0)[None, :, None]
    k = np.array([2.0, 4.0])[rng.permutation(8) % 2]
    x = np.zeros((N, 8, 16, C, 4))
    u = d["u"].astype(np.float32).reshape(N, 128, 128, 4)
    v = np.zeros((N, 128, 512), np.float32)
    w = np.zeros((N, 128, 4, 128, 4), np.float32)
    i = np.arange(128)
    for r in range(N):
        low = -0.7 * (0.9 + 0.1 * rng.random((8, 16, C, 4))) * 2.0 ** 30
        tiny = -(1.0 + 0.125 * rng.integers(0, 8, (8, 16, C, 4))) * 2.0 ** -30
        if o[r] == 0: x[r] = low
        if o[r] == 1: x[r] = np.where((rng.random(C) < 0.5)[:, None], 0.7 * (1.0 + 0.4 * rng.random((8, 16, C, 4))) * 2.0 ** 27, low)
        if o[r] == 2: x[r] = tiny
        if o[r] == 3: x[r] = d["x"][r].astype(np.float32).reshape(8, 16, C, 4)[:, :, :1]
        x[r, e, 8:] = tiny[e, 8:, :1] if o[r] == 3 else tiny[e, 8:]
        if o[r] < 2: u[r, :, ::16] = c * (0.9 + 0.1 * rng.random((128, 8, 4))) * 2.0 ** 30
        if o[r] == 2: u[r, :, ::16] = c * (1.0 + 0.125 * rng.integers(0, 8, (128, 8, 4))) * 2.0 ** -30
        if o[r] == 3: u[r, :, ::16] *= np.abs(c).astype(np.float32)
        a = (0.9 + 0.1 * rng.random((128, 512))) * 2.0 ** 30 if o[r] < 2 else (1.0 + 0.125 * rng.integers(0, 8, (128, 512))) * 2.0 ** -30
        v[r] = rng.choice([-1.0, 1.0], (128, 512)) * a
        t = k[i // 16]
        t[16 * e + 8:16 * e + 16] = 2.0 ** 8 if most[r] else 2.0 ** -8
        for b in range(4): w[r, i, b, i, b] = t
    return {"x": x.astype(np.float32).reshape(N, 128, 4 * C).astype(BF), "u": u.reshape(N, 128, 512).astype(BF), "v": v.astype(BF), **rings(rng), **weights(rng, w.astype(BF))}
def setup_inputs_spread(rng):
    d = setup_inputs(rng)
    d["x"] = wide(rng, N, 128, 4 * C, cols=6)
    return d
def check_inputs(d):
    b = []
    for k in ("x", "u", "v"):
        a = np.abs(d[k].astype(np.float32))
        if not (np.isfinite(a).all() and ((a == 0) | (a >= 2.0 ** -30) & (a <= 2.0 ** 30)).all()): b.append("a value of " + k)
    none, least, most = [emit(mx_ref.quantize(np.full((128, 16), k, np.float32).astype(BF)))[1][0, 0] for k in (0.0, 2.0 ** -8, 2.0 ** 8)]
    for r in range(N):
        if not (np.sort(gentries(d["od"][r]), axis=1) == np.arange(C)).all(): b.append("od: a group whose entries are not all columns once")
        if ((d["wc"][r] == 0x7F) | (d["wc"][r] == 0xFF)).any(): b.append("wc: a code that is no number")
        s = mx_ref.live(d["ws"][r])
        if ((s != none) & ((s < least) | (s > most))).any(): b.append("ws: a scale out of range")
        if (((d["wc"][r].reshape(16, 8, 512, 4) & 0x7F) != 0) & (s == none)[:, None, :, None]).any(): b.append("wc: a code other than zero under the scale of zeros")
    return b
def at(t, e):
    return np.take_along_axis(t, e, axis=1)
def reference(x, u, v, od, wc, ws):
    qu = [mx_ref.quantize(u[r]) for r in range(N)]
    lay = [pk(wc[r], ws[r]) for r in range(N)]
    now = [x[r] for r in range(N)]
    order = [gentries(od[r]).astype(np.int64) for r in range(N)]
    for step in STEP:
        old, order, far, z = order, [], [], []
        for r in range(N):
            q = mx_ref.quantize(now[r])
            s = mx_ref.matmul(qu[r], q)[::16]
            mine, other = old[r], old[r ^ step]
            jump = at(np.argsort(other, axis=1), mine)
            low = np.tile(np.arange(C), (8, 1))
            for i in range(9):
                low = np.minimum(low, at(low, jump))
                jump = at(jump, jump)
            order.append(np.where(at(s, at(mine, low)) > 0, other, mine))
            far.append(decode(q))
            t = far[r].astype(BF)
            pair = gcols(t, order[r]).astype(np.float32) + gcols(t, at(order[r], order[r])).astype(np.float32)
            z.append(mx_ref.quantize((pair * np.float32(0.5)).astype(BF)))
        for r in range(N):
            back = np.argsort(order[r], axis=1)
            now[r] = tile([gpick(mx_ref.matmul(pick(lay[r], np.arange(128 * b, 128 * b + 128)), z[r ^ step]) * np.float32(0.03125), back) + far[r][:, b::4] for b in range(4)])
    y, fo = np.zeros((N, 128, C), np.float32), np.zeros((N, 8, C), np.float32)
    oc, osc = np.zeros((N, 128, 4 * C), np.uint8), np.zeros((N, 16, C), np.uint8)
    for r in range(N):
        q = mx_ref.quantize(now[r])
        y[r] = mx_ref.matmul(mx_ref.quantize(v[r]), q)
        fo[r] = order[r]
        oc[r], osc[r] = emit(q)
    return {"y": y, "fo": fo, "oc": oc, "osc": osc}

@@ -1,0 +1,417 @@
+from concourse.bass import DstId, RemoteDMATransfer
+from concourse.mybir import dt, AluOpType, ActivationFunctionType
+
+C = 288
+STEP = [4, 1, 2]
+RAD = [2, 2, 2, 2, 2, 3, 3]
+SUMMED = (0, 2)
+F32, BF, I32, U16, U8, MX = "float32", "bfloat16", "int32", "uint16", "uint8", "float8_e4m3fn_x4"
+
+
+def _scratch():
+    s = {}
+
+    def sb(dtype, **names):
+        for k in names: s[k] = ("sbuf", [128, names[k]], dtype)
+    sb(I32, odi=18, bi=18, hod=18, ivi=18, bv=18, hiv=18, pidx=1, p15=1, zki=36, zkm=36)
+    sb(U16, ofc=36, uof=8, b0=18, ll=36)
+    for k in range(4): sb(U16, **{"aw%d" % k: 36})
+    for k in (1, 2): sb(U16, **{a + "%d" % k: 18 for a in ("hw", "bw", "hx", "bx")})
+    for k in range(len(RAD)): sb(U16, **{"lo%d" % k: 18})
+    sb(BF, xin=4 * C, uin=512, vin=512, et=2048, zt=4 * C, xt=4 * C)
+    sb(BF, ci=C, scc=2 * C, ivr=C, ja=C, jb=C, jc=C, zj=C, fl=C, tf=2 * C, zf=2 * C)
+    for k in (1, 2): sb(BF, **{"op%d" % k: C})
+    sb(F32, iot=512, i5=C, p4=4, p16=1, sct=1, scol=1, ne=16, nx=16, t1=16, t2=16, sc16=16, dk16=16, dkk=2 * C)
+    sb(F32, k0=C, k1=C, k2=C, c0=C, c1=C, gs=4 * C, kk=2 * C, zk=2 * C, bf=36, df=36, ds=36, fw=36, fm=36, af0=36, af1=36, af2=36, af3=36)
+    sb(F32, fs=4 * C, ys=4 * C, fp=4 * C, rr=4 * C, yo=C, fr=C)
+    for k, n in (("w", 512), ("e", 512), ("u", 128), ("ur", 128), ("v", 128)): sb(MX, **{k + "q": n}); sb(U8, **{k + "p": n})
+    for k in range(4): sb(MX, **{"xq%d" % k: C}); sb(U8, **{"xs%d" % k: C})
+    for k in range(3):
+        for a in "zhr": sb(MX, **{"%sq%d" % (a, k): C}); sb(U8, **{"%ss%d" % (a, k): C})
+    s["pd"] = ("psum", [128, 2048], F32)
+    s["pr"] = ("psum", [128, 2048], F32)
+    return s
+
+
+SCRATCH = _scratch()
+SEMAPHORES = ["cv", "cs", "ct", "cg", "lod", "lx", "lu", "lv", "lwc", "lws", "store", "sent",
+              "hod", "hiv", "hw1", "hw2", "hx1", "hx2", "rx1", "rx2", "hq0", "hq1", "hq2", "hs0", "hs1", "hs2",
+              "roda", "rivb", "rivc", "rw1", "rw2", "rqa0", "rqa1", "rqa2", "rqb0", "rqb1", "rqb2", "rs0", "rs1", "rs2"]
+
+
+def _mask(es):
+    return sum(1 << e for e in es)
+
+
+def _helpers(rc, dest, topo):
+    h = [c for c in topo.cores_of(rc) if c != rc and topo.may_write(c, dest)]
+    near = [c for c in h if topo.die(c) == topo.die(rc)]
+    far = [c for c in h if topo.die(c) != topo.die(rc)]
+    return near[0], far[0], near[1]
+
+
+def _relay(g, core, rc, T, topo):
+    rank, n = T.rank_of(rc), 0
+
+    def fwd(dest, dst, src, sem):
+        rid, pid = topo.addr(dest, core)
+        g.remote_dma(out_ap=dst, in_ap=src, remote_sem=T.sem[sem], local_sem=T.sem["sent"], pid=pid, routing_id=rid, dma_engine_mask=topo.mask(core, dest))
+        return len(topo.engines(core, dest))
+
+    def on_chip(k):
+        return len(topo.engines(rc, core)) // k
+    dests = [T.cores[rank ^ s] for s in STEP]
+    for t, dest in enumerate(dests):
+        a, b, c = _helpers(rc, dest, topo)
+        if t == 0:
+            if core == a:
+                g.wait_ge(T.sem["hod"], on_chip(2))
+                n += fwd(dest, T["bi"][:, :], T["hod"][:, :], "roda")
+            for h, lo, sem in ((b, 0, "rivb"), (c, 9, "rivc")):
+                if core == h:
+                    g.wait_ge(T.sem["hiv"], on_chip(4))
+                    n += fwd(dest, T["bv"][:, lo:lo + 9], T["hiv"][:, lo:lo + 9], sem)
+        if t < 2 and core == _helpers(rc, dests[t + 1], topo)[0]:
+            k = "w%d" % (t + 1)
+            g.wait_ge(T.sem["h" + k], on_chip(1))
+            n += fwd(dests[t + 1], T["b" + k][:, :], T["h" + k][:, :], "r" + k)
+        for h, lo, sem in ((a, 0, "rqa"), (b, C // 2, "rqb")):
+            if core == h:
+                k = "q%d" % t
+                g.wait_ge(T.sem["h" + k], on_chip(2))
+                n += fwd(dest, T["r" + k][:, lo:lo + C // 2].bitcast(dt.uint8), T["h" + k][:, lo:lo + C // 2].bitcast(dt.uint8), "%s%d" % (sem, t))
+        if core == c:
+            k = "s%d" % t
+            g.wait_ge(T.sem["h" + k], on_chip(1))
+            n += fwd(dest, T["r" + k][:, :], T["h" + k][:, :], "r" + k)
+        if t < 2 and core == _helpers(rc, dests[t + 1], topo)[2]:
+            k = "x%d" % (t + 1)
+            g.wait_ge(T.sem["h" + k], on_chip(1))
+            n += fwd(dests[t + 1], T["b" + k][:, :], T["h" + k][:, :], "r" + k)
+    if n: g.wait_ge(T.sem["sent"], n)
+
+
+def rank_program(g, core, T, topo):
+    rank = T.rank_of(core)
+    if rank is None:
+        for c in topo.cores_of(core):
+            if T.rank_of(c) is not None: _relay(g, core, c, T, topo)
+        return
+    A = AluOpType
+    COPY, RELU, SIGN = ActivationFunctionType.Copy, ActivationFunctionType.Relu, ActivationFunctionType.Sign
+    eng = {"v": g.vector, "s": g.scalar, "t": g.tensor, "y": g.sync, "g": g}
+    count, last_write, readers = {}, {}, {}
+    known = {q: {} for q in eng}
+
+    def settle(q, events):
+        best = {}
+        for s, n, snap in events:
+            if known[q].get(s, 0) < n and (s not in best or best[s][0] < n): best[s] = (n, snap)
+        for s in list(best):
+            if any(o != s and best[o][1].get(s, 0) >= best[s][0] for o in best): del best[s]
+        for s in best:
+            n, snap = best[s]
+            eng[q].wait_ge(T.sem[s], n)
+            for k, m in list(snap.items()) + [(s, n)]: known[q][k] = max(known[q].get(k, 0), m)
+
+    def call(q, make, reads, writes, sem=None, step=1):
+        banks = [r for r in reads if r[:2] in ("pd", "pr")]
+        events = []
+        for r in reads: events += last_write.get(r, [])
+        for r in writes + banks: events += last_write.get(r, []) + readers.get(r, [])
+        settle(q, events)
+        ins = make(eng[q])
+        s = sem or "c" + q
+        count[s] = count.get(s, 0) + step
+        ins.then_inc(T.sem[s], step)
+        e = (s, count[s], dict(known[q]))
+        for r in reads: readers.setdefault(r, []).append(e)
+        for r in writes: last_write[r], readers[r] = [e], []
+
+    def arrived(regions, *events):
+        for r in regions: last_write[r], readers[r] = [(s, n, {}) for s, n in events], []
+
+    def load(q, dst, src, sem, writes): call(q, lambda e: e.dma_start(dst, src), [], writes, sem, 16)
+
+    def store(q, dst, src, reads): call(q, lambda e: e.dma_start(dst, src), reads, [], "store", 16)
+
+    def tt(out, in0, in1, op, reads, writes): call("v", lambda e: e.tensor_tensor(out, in0, in1, op), reads, writes)
+
+    def ts(out, in0, s1, s2, op0, op1, reads, writes):
+        if op1 is None: call("v", lambda e: e.tensor_scalar(out, in0, s1, None, op0), reads, writes)
+        else: call("v", lambda e: e.tensor_scalar(out, in0, s1, s2, op0, op1), reads, writes)
+
+    def vcopy(out, in_, reads, writes): call("v", lambda e: e.tensor_copy(out, in_), reads, writes)
+
+    def scopy(out, in_, reads, writes, scale=1.0):
+        if scale == 1.0: call("s", lambda e: e.activation(out, in_, COPY), reads, writes)
+        else: call("s", lambda e: e.activation(out, in_, COPY, scale=scale), reads, writes)
+
+    def scan(out, d0, d1, op0, op1, reads, writes): call("v", lambda e: e.tensor_tensor_scan(out, d0, d1, 0.0, op0, op1), reads, writes)
+
+    def quant(q, s, in_, reads, writes): call("v", lambda e: e.quantize_mx(q, s, in_), reads, writes)
+
+    def mm(out, lq, ls, rq, rs, reads, writes): call("t", lambda e: e.matmul_mx(out, lq, ls, rq, rs, True, True), reads, writes)
+
+    sent = [0]
+    dests = [T.cores[rank ^ s] for s in STEP]
+    back = [[len(topo.engines(h, core)) for h in _helpers(d, core, topo)] for d in dests]
+
+    def send(reads, *parts):
+        settle("g", [e for r in reads for e in last_write.get(r, [])])
+        if len(parts) == 1:
+            h, dst, src, sem, es = parts[0]
+            rid, pid = topo.addr(h, core)
+            g.remote_dma(out_ap=dst, in_ap=src, remote_sem=T.sem[sem], local_sem=T.sem["sent"], pid=pid, routing_id=rid, dma_engine_mask=_mask(es))
+        else:
+            moves = []
+            for h, dst, src, sem, es in parts:
+                rid, pid = topo.addr(h, core)
+                moves.append(RemoteDMATransfer(dst_ids=[DstId(rid=rid, pnc=pid)], dma_engine_mask=_mask(es), remote_sem=T.sem[sem], src=src, dst=dst))
+            g.remote_dma_fused(moves, local_sem=T.sem["sent"])
+        sent[0] += sum(len(p[4]) for p in parts)
+
+    load("y", T["odi"][:, :], T.od[:, :], "lod", ["odi"])
+    load("s", T["xin"][:, :], T.x[:, :], "lx", ["xin"])
+    load("y", T["uin"][:, :], T.u[:, :], "lu", ["uin"])
+    load("y", T["wq"][:, :].bitcast(dt.uint8), T.wc[:, :], "lwc", ["wq"])
+    load("y", T["wp"][:, :], T.ws[:, :], "lws", ["wp"])
+    load("y", T["vin"][:, :], T.v[:, :], "lv", ["vin"])
+    ha, hb, hc = _helpers(core, dests[0], topo)
+    es = topo.engines(core, ha)
+    iot, ci = T["iot"], T["ci"]
+    call("g", lambda e: e.iota(iot[:, :], [[1, 512]], 0, 0, allow_small_or_imprecise_dtypes=True), [], ["iot"])
+    call("g", lambda e: e.iota(T["pidx"][:, :], [[1, 1]], 0, 1), [], ["pidx"])
+    call("g", lambda e: e.iota(T["p4"][:, :], [[1, 4]], 0, 4, allow_small_or_imprecise_dtypes=True), [], ["p4"])
+    send(["odi"], (ha, T["hod"][:, :], T["odi"][:, :], "hod", es[1::2]))
+    arrived(["bi"], ("roda", back[0][0]))
+    arrived(["bv"], ("rivb", back[0][1]), ("rivc", back[0][2]))
+    for t in range(3):
+        if t:
+            arrived(["bw%d" % t], ("rw%d" % t, back[t][0]))
+            arrived(["bx%d" % t], ("rx%d" % t, back[t][2]))
+        arrived(["rz%d" % t], ("rqa%d" % t, back[t][0]), ("rqb%d" % t, back[t][1]), ("rs%d" % t, back[t][2]))
+
+    ts(ci[:, :], iot[:, 0:C], -144.0, None, A.add, None, ["iot"], ["ci"])
+    ts(T["p15"][:, :], T["pidx"][:, :], 15, None, A.bitwise_and, None, ["pidx"], ["p15"])
+    vcopy(T["p16"][:, :], T["p15"][:, :], ["p15"], ["p16"])
+    ts(T["ofc"][:, :], iot[:, 0:36], 0.0, T["p16"][:, :], A.mult, A.add, ["iot", "p16"], ["ofc"])
+    ts(T["ne"][:, :], iot[:, 0:16], T["p16"][:, :], None, A.not_equal, None, ["iot", "p16"], ["ne"])
+    ts(T["nx"][:, :], iot[:, 0:16], T["p16"][:, :], 1.0, A.subtract, A.is_equal, ["iot", "p16"], ["nx"])
+    ts(T["t1"][:, :], T["nx"][:, :], 1048575.0, None, A.mult, None, ["nx"], ["t1"])
+    tt(T["sc16"][:, :], T["t1"][:, :], T["ne"][:, :], A.add, ["t1", "ne"], ["sc16"])
+    ts(T["sct"][:, :], T["p16"][:, :], 15.0, 1.0 - 2.0 ** -20, A.is_equal, A.mult, ["p16"], ["sct"])
+    ts(T["scol"][:, :], T["sct"][:, :], 2.0 ** -20, None, A.add, None, ["sct"], ["scol"])
+    scopy(T["scc"][:, :], T["sc16"][:, :].indirect(T["ofc"][:, :]), ["sc16", "ofc"], ["scc"])
+
+    def wrap(src, out, writes):
+        scan(T["zj"][:, :], T["scc"][:, 0:C], T[src][:, :], A.mult, A.add, ["scc", src], ["zj"])
+        ts(out, T["zj"][:, 15:C:16], T["scol"][:, :], 144.25, A.mult, A.add, ["zj", "scol"], writes)
+
+    vcopy(T["aw0"][:, 18:36], T["odi"][:, :], ["odi"], ["aw0.o"])
+    vcopy(T["ivr"][:, :].indirect(T["aw0"][:, 18:36]), ci[:, :], ["ci", "aw0.o"], ["ivr"])
+    wrap("ivr", T["aw0"][:, 0:18], ["aw0.i"])
+    vcopy(T["ivi"][:, :], T["aw0"][:, 0:18], ["aw0.i"], ["ivi"])
+    send(["ivi"], (hb, T["hiv"][:, 0:9], T["ivi"][:, 0:9], "hiv", es[0::4]), (hc, T["hiv"][:, 9:18], T["ivi"][:, 9:18], "hiv", es[2::4]))
+
+    def off(t, k):
+        return T["aw%d" % t][:, 0:18] if k == "i" else T["aw%d" % t][:, 18:36]
+
+    def keys(t):
+        tt(T["k0"][:, :], T["i5"][:, :].indirect(off(t, "i")), iot[:, 0:C], A.add, ["i5", "aw%d.i" % t, "iot"], ["k0"])
+
+    def bank(p, b, n=C): return T[p][:, 512 * b:512 * b + n]
+
+    def part(name, b): return T[name][:, C * b:C * b + C]
+
+    def score(t):
+        q, s = T["xq%d" % t], T["xs%d" % t]
+        mm(bank("pr", 0), T["urq"][:, :], T["urp"][:, :], q[:, :], s[:, :], ["urq", "urp", "x%d" % t], ["pr0"])
+
+    def unpack(t, b):
+        q, s = T["xq%d" % t], T["xs%d" % t]
+        mm(bank("pd", b), T["eq"][:, 128 * b:128 * b + 128], T["ep"][:, 128 * b:128 * b + 128], q[:, :], s[:, :], ["e", "x%d" % t], ["pd%d" % b])
+
+    def held(b): scopy(part("fs", b), bank("pd", b), ["pd%d" % b], ["fs%d" % b])
+
+    def signs(): call("s", lambda e: e.activation(T["fl"][:, :], bank("pr", 0), SIGN), ["pr0"], ["fl"])
+
+    def shifted(out, in_, reads, writes): ts(out, in_, 0.25, None, A.add, None, reads, writes)
+
+    def chase(t, mid):
+        if t == 0:
+            vcopy(T["b0"][:, :], T["bi"][:, :], ["bi"], ["b0"])
+            scopy(T["jb"][:, :], ci[:, :].indirect(T["b0"][:, :]), ["ci", "b0"], ["jb"])
+            scopy(T["ja"][:, :], T["jb"][:, :].indirect(off(0, "i")), ["jb", "aw0.i"], ["ja"])
+        else:
+            scopy(T["ja"][:, :], T["op%d" % t][:, :].indirect(T["bw%d" % t][:, 0:18]), ["op%d" % t, "bw%d" % t], ["ja"])
+        scopy(T["c0"][:, :], T["k0"][:, :], ["k0"], ["c0"])
+        wrap("ja", T["lo0"][:, :], ["lo0"])
+        jr, key, twin = "ja", "k0", "c0"
+        for i, r in enumerate(RAD):
+            last = i == len(RAD) - 1
+            lo = "lo%d" % i
+            if not last:
+                src = jr
+                for m in range(r - 1):
+                    dst = [x for x in ("ja", "jb", "jc") if x not in (src, jr)][0]
+                    scopy(T[dst][:, :], T[src][:, :].indirect(T[lo][:, :]), [src, lo], [dst])
+                    src = dst
+            acc = key
+            for m in range(r - 1):
+                if last and m == r - 2: name, out = "kk0", T["kk"][:, 0:C]
+                else:
+                    name = [x for x in ("k0", "k1", "k2") if x not in (acc, key)][0]
+                    out = T[name][:, :]
+                tt(out, T[acc][:, :].indirect(T[lo][:, :]), T[twin][:, :], A.min, [acc, twin, lo], [name])
+                acc = name
+                if last and m == 0: mid()
+            key = acc
+            if not last:
+                twin = "c1" if twin == "c0" else "c0"
+                scopy(T[twin][:, :], T[key][:, :], [key], [twin])
+                jr = src
+                wrap(jr, T["lo%d" % (i + 1)][:, :], ["lo%d" % (i + 1)])
+
+    def spread(h):
+        k, a, b = str(h), C * h, C * h + C
+        scan(T["zk"][:, a:b], T["dkk"][:, a:b], T["kk"][:, a:b], A.add, A.max, ["dkk", "kk" + k], ["zk" + k])
+
+    def choose(t):
+        n = t + 1
+        af, aw = "af%d" % t, "aw%d" % n
+
+        def leaders(h):
+            k = str(h)
+            a, b = 18 * h, 18 * h + 18
+            vcopy(T["zki"][:, a:b], T["zk"][:, C * h + 15:C * h + C:16], ["zk" + k], ["zki" + k])
+            ts(T["zkm"][:, a:b], T["zki"][:, a:b], 511, None, A.bitwise_and, None, ["zki" + k], ["zkm" + k])
+            vcopy(T["ll"][:, a:b], T["zkm"][:, a:b], ["zkm" + k], ["ll" + k])
+
+        def flags(h):
+            k = str(h)
+            call("s", lambda e: e.activation(T["tf"][:, C * h:C * h + C], T["fl"][:, :].indirect(T["ll"][:, 18 * h:18 * h + 18]), RELU), ["fl", "ll" + k], ["tf" + k])
+
+        def take(h):
+            k, r = str(h), aw + (".i", ".o")[h]
+            a, b = C * h, C * h + C
+            scan(T["zf"][:, a:b], T["scc"][:, a:b], T["tf"][:, a:b], A.mult, A.add, ["scc", "tf" + k], ["zf" + k])
+            a, b = 18 * h, 18 * h + 18
+            tt(T["fm"][:, a:b], T["zf"][:, C * h + 15:C * h + C:16], T["ds"][:, a:b], A.mult, ["zf" + k, "ds"], ["fm" + k])
+            tt(T["fw"][:, a:b], T["fm"][:, a:b], T[af][:, a:b], A.add, ["fm" + k, af], ["fw" + k])
+            vcopy(T[aw][:, a:b], T["fw"][:, a:b], ["fw" + k], [r])
+        scopy(T["kk"][:, C:2 * C], T["kk"][:, 0:C].indirect(off(t, "o")), ["kk0", "aw%d.o" % t], ["kk1"])
+        leaders(0)
+        signs()
+        if t == 0:
+            shifted(T["bf"][:, 0:18], T["bv"][:, :], ["bv"], ["bf.i"])
+            shifted(T["bf"][:, 18:36], T["bi"][:, :], ["bi"], ["bf.o"])
+        else:
+            shifted(T["bf"][:, 0:18], T["bw%d" % t][:, :], ["bw%d" % t], ["bf.i"])
+            shifted(T["bf"][:, 18:36], T["bx%d" % t][:, :], ["bx%d" % t], ["bf.o"])
+        tt(T["df"][:, :], T["bf"][:, :], T[af][:, :], A.subtract, ["bf.i", "bf.o", af], ["df"])
+        ts(T["ds"][:, :], T["df"][:, :], T["scol"][:, :], None, A.mult, None, ["df", "scol"], ["ds"])
+        flags(0)
+        spread(1)
+        leaders(1)
+        if t: held(0)
+        flags(1)
+        take(0)
+        if n < 3: send([aw + ".i"], (_helpers(core, dests[n], topo)[0], T["hw%d" % n][:, :], T[aw][:, 0:18], "hw%d" % n, es))
+        take(1)
+        if t:
+            for b in (1, 2): held(b)
+
+    def means(t):
+        n = t + 1
+        o, ro = off(n, "o"), "aw%d.o" % n
+
+        def pair(b): tt(part("ys", b), part("gs", b), bank("pd", b), A.add, ["gs%d" % b, "pd%d" % b], ["ys%d" % b])
+        for b in (1, 2, 3):
+            scopy(part("gs", b), part("fs", b).indirect(o), ["fs%d" % b, ro], ["gs%d" % b])
+            if t and b == 1: held(3)
+        vcopy(part("gs", 0), part("fs", 0).indirect(o), ["fs0", ro], ["gs0"])
+        for k, b in ("y1", "y0", "z1", "y2", "y3", "z2"):
+            b = int(b)
+            if k == "y": pair(b)
+            else: ts(T["zt"][:, b:4 * C:4], part("ys", b).indirect(o), 0.5, None, A.mult, None, ["ys%d" % b, ro], ["zt%d" % b])
+        for b in (0, 3): scopy(T["zt"][:, b:4 * C:4], part("ys", b).indirect(o), ["ys%d" % b, ro], ["zt%d" % b], 0.5)
+        zq, zs = T["zq%d" % t], T["zs%d" % t]
+        quant(zq[:, :], zs[:, :], T["zt"][:, :], ["zt0", "zt1", "zt2", "zt3"], ["z%d" % t])
+        a, b, c = _helpers(core, dests[t], topo)
+        hq, h = T["hq%d" % t], C // 2
+        send(["z%d" % t], (a, hq[:, 0:h].bitcast(dt.uint8), zq[:, 0:h].bitcast(dt.uint8), "hq%d" % t, es[1::2]),
+             (b, hq[:, h:C].bitcast(dt.uint8), zq[:, h:C].bitcast(dt.uint8), "hq%d" % t, es[0::2]))
+        send(["z%d" % t], (c, T["hs%d" % t][:, :], zs[:, :], "hs%d" % t, es))
+        if n < 3:
+            send([ro], (_helpers(core, dests[n], topo)[2], T["hx%d" % n][:, :], o, "hx%d" % n, es))
+            scopy(T["op%d" % n][:, :], ci[:, :].indirect(o), ["ci", ro], ["op%d" % n])
+            keys(n)
+            shifted(T["af%d" % n][:, :], T["aw%d" % n][:, :], ["aw%d.i" % n, "aw%d.o" % n], ["af%d" % n])
+        for b in SUMMED: scopy(part("fp", b), part("fs", b).indirect(o), ["fs%d" % b, ro], ["fp%d" % b], 32.0)
+
+    def products(t):
+        n = t + 1
+        i, ri = off(n, "i"), "aw%d.i" % n
+        rq, rs = T["rq%d" % t], T["rs%d" % t]
+        for b in range(4):
+            mm(bank("pr", b), T["wq"][:, 128 * b:128 * b + 128], T["wp"][:, 128 * b:128 * b + 128], rq[:, :], rs[:, :], ["wq", "wp", "rz%d" % t], ["pr%d" % b])
+        for b in SUMMED: tt(part("rr", b), bank("pr", b), part("fp", b), A.add, ["pr%d" % b, "fp%d" % b], ["rr%d" % b])
+
+        def scaled(b): scopy(part("rr", b), bank("pr", b), ["pr%d" % b], ["rr%d" % b], 0.03125)
+
+        def moved(b): scopy(T["xt"][:, b:4 * C:4], part("rr", b).indirect(i), ["rr%d" % b, ri], ["xt%d" % b], 0.03125)
+        for f, b in ((scaled, 1), (moved, 0), (scaled, 3), (moved, 2)): f(b)
+
+    def state(t):
+        n = t + 1
+        i, ri = off(n, "i"), "aw%d.i" % n
+        for b in range(4):
+            if b not in SUMMED: tt(T["xt"][:, b:4 * C:4], part("rr", b).indirect(i), part("fs", b), A.add, ["rr%d" % b, ri, "fs%d" % b], ["xt%d" % b])
+        if n < 3: spread(0)
+        quant(T["xq%d" % n][:, :], T["xs%d" % n][:, :], T["xt"][:, :], ["xt0", "xt1", "xt2", "xt3"], ["x%d" % n])
+        if n < 3:
+            score(n)
+            for b in range(4): unpack(n, b)
+
+    ts(T["t1"][:, :], T["ne"][:, :], 1.0, 2.0 ** 20, A.subtract, A.mult, ["ne"], ["t1"])
+    ts(T["t2"][:, :], T["nx"][:, :], 2.0 ** 18, None, A.mult, None, ["nx"], ["t2"])
+    tt(T["dk16"][:, :], T["t1"][:, :], T["t2"][:, :], A.add, ["t1", "t2"], ["dk16"])
+    scopy(T["dkk"][:, :], T["dk16"][:, :].indirect(T["ofc"][:, :]), ["dk16", "ofc"], ["dkk"])
+    ts(T["i5"][:, :], iot[:, 0:C], 512.0, None, A.mult, None, ["iot"], ["i5"])
+    keys(0)
+    ts(T["uof"][:, :], iot[:, 0:8], 16.0, None, A.mult, None, ["iot"], ["uof"])
+    for b in range(4): ts(T["et"][:, 512 * b:512 * b + 512], iot[:, :], T["p4"][:, b:b + 1], None, A.is_equal, None, ["iot", "p4"], ["et%d" % b])
+    quant(T["eq"][:, :], T["ep"][:, :], T["et"][:, :], ["et0", "et1", "et2", "et3"], ["e"])
+    quant(T["xq0"][:, :], T["xs0"][:, :], T["xin"][:, :], ["xin"], ["x0"])
+    for b in range(4): unpack(0, b)
+    for b in range(4): held(b)
+    quant(T["uq"][:, :], T["up"][:, :], T["uin"][:, :], ["uin"], ["u"])
+    vcopy(T["urq"][:, :].bitcast(dt.uint32), T["uq"][:, :].bitcast(dt.uint32).indirect(T["uof"][:, :]), ["u", "uof"], ["urq"])
+    vcopy(T["urp"][:, :], T["up"][:, :].indirect(T["uof"][:, :]), ["u", "uof"], ["urp"])
+    score(0)
+    shifted(T["af0"][:, :], T["aw0"][:, :], ["aw0.i", "aw0.o"], ["af0"])
+    chase(0, lambda: None)
+    spread(0)
+    choose(0)
+    means(0)
+    for t in (1, 2):
+        chase(t, lambda: products(t - 1))
+        state(t - 1)
+        choose(t)
+        means(t)
+    quant(T["vq"][:, :], T["vp"][:, :], T["vin"][:, :], ["vin"], ["v"])
+    vcopy(T["fr"][:, :], iot[:, 0:C].indirect(off(3, "o")), ["iot", "aw3.o"], ["fr"])
+    for k in range(8): store("y", T.fo[k:k + 1, :], T["fr"][16 * k:16 * k + 1, :], ["fr"])
+    products(2)
+    state(2)
+    store("y", T.oc[:, :], T["xq3"][:, :].bitcast(dt.uint8), ["x3"])
+    h = C // 2
+    for k in range(2): mm(bank("pr", k, h), T["vq"][:, :], T["vp"][:, :], T["xq3"][:, h * k:h * k + h], T["xs3"][:, h * k:h * k + h], ["v", "x3"], ["pr%d" % k])
+    for k in range(4): store("y" if k < 2 else "s", T.osc[4 * k:4 * k + 4, :], T["xs3"][32 * k:32 * k + 4, :], ["x3"])
+    vcopy(T["yo"][:, 0:h], bank("pr", 0, h), ["pr0"], ["yo0"])
+    scopy(T["yo"][:, h:C], bank("pr", 1, h), ["pr1"], ["yo1"])
+    store("y", T.y[:, 0:h], T["yo"][:, 0:h], ["yo0"])
+    store("s", T.y[:, h:C], T["yo"][:, h:C], ["yo1"])
+    for s in ("cv", "cs", "ct", "cg", "store"): g.wait_ge(T.sem[s], count[s])
+    g.wait_ge(T.sem["sent"], sent[0])

@@ -4,7 +4,6 @@ from concourse.mybir import dt, AluOpType, ActivationFunctionType
 C = 288
 STEP = [4, 1, 2]
 RAD = [2, 2, 2, 2, 2, 3, 3]
-SUMMED = (0, 2)
 F32, BF, I32, U16, U8, MX = "float32", "bfloat16", "int32", "uint16", "uint8", "float8_e4m3fn_x4"
 
 
@@ -13,17 +12,17 @@ def _scratch():
 
     def sb(dtype, **names):
         for k in names: s[k] = ("sbuf", [128, names[k]], dtype)
-    sb(I32, odi=18, bi=18, hod=18, ivi=18, bv=18, hiv=18, pidx=1, p15=1, zki=36, zkm=36)
-    sb(U16, ofc=36, uof=8, b0=18, ll=36)
+    sb(I32, odi=18, bi=18, hod=18, ivi=18, bv=18, hiv=18, pidx=1, p15=1)
+    sb(U16, ofc=18, uof=8, b0=18, ll=18)
     for k in range(4): sb(U16, **{"aw%d" % k: 36})
     for k in (1, 2): sb(U16, **{a + "%d" % k: 18 for a in ("hw", "bw", "hx", "bx")})
     for k in range(len(RAD)): sb(U16, **{"lo%d" % k: 18})
     sb(BF, xin=4 * C, uin=512, vin=512, et=2048, zt=4 * C, xt=4 * C)
-    sb(BF, ci=C, scc=2 * C, ivr=C, ja=C, jb=C, jc=C, zj=C, fl=C, tf=2 * C, zf=2 * C)
-    for k in (1, 2): sb(BF, **{"op%d" % k: C})
-    sb(F32, iot=512, i5=C, p4=4, p16=1, sct=1, scol=1, ne=16, nx=16, t1=16, t2=16, sc16=16, dk16=16, dkk=2 * C)
-    sb(F32, k0=C, k1=C, k2=C, c0=C, c1=C, gs=4 * C, kk=2 * C, zk=2 * C, bf=36, df=36, ds=36, fw=36, fm=36, af0=36, af1=36, af2=36, af3=36)
-    sb(F32, fs=4 * C, ys=4 * C, fp=4 * C, rr=4 * C, yo=C, fr=C)
+    sb(BF, ci=C, scc=C, ja=C, jb=C, jc=C, zj=C, zk=C, k0=C, k1=C, k2=C, c0=C, c1=C, fl=C, flp=C, tf0=C, tf1=C, zf0=C, zf1=C)
+    for k in range(3): sb(BF, **{"iw%d" % k: C})
+    sb(F32, iot=C, p1=1, p16=1, sct=1, scol=1, ne=16, nx=16, t1=16, sc16=16)
+    sb(F32, gs=4 * C, bf=36, df=36, ds=36, fw=36, fm=36, af0=36, af1=36, af2=36)
+    sb(F32, fs=4 * C, ys=4 * C, rr=4 * C, yo=C, fr=C)
     for k, n in (("w", 512), ("e", 512), ("u", 128), ("ur", 128), ("v", 128)): sb(MX, **{k + "q": n}); sb(U8, **{k + "p": n})
     for k in range(4): sb(MX, **{"xq%d" % k: C}); sb(U8, **{"xs%d" % k: C})
     for k in range(3):
@@ -34,7 +33,7 @@ def _scratch():
 
 
 SCRATCH = _scratch()
-SEMAPHORES = ["cv", "cs", "ct", "cg", "lod", "lx", "lu", "lv", "lwc", "lws", "store", "sent",
+SEMAPHORES = ["cv", "cs", "ct", "cg", "lod", "lx", "lu", "lv", "lwc", "lws", "store", "sent", "sod",
               "hod", "hiv", "hw1", "hw2", "hx1", "hx2", "rx1", "rx2", "hq0", "hq1", "hq2", "hs0", "hs1", "hs2",
               "roda", "rivb", "rivc", "rw1", "rw2", "rqa0", "rqa1", "rqa2", "rqb0", "rqb1", "rqb2", "rs0", "rs1", "rs2"]
 
@@ -71,10 +70,11 @@ def _relay(g, core, rc, T, topo):
                 if core == h:
                     g.wait_ge(T.sem["hiv"], on_chip(4))
                     n += fwd(dest, T["bv"][:, lo:lo + 9], T["hiv"][:, lo:lo + 9], sem)
-        if t < 2 and core == _helpers(rc, dests[t + 1], topo)[0]:
-            k = "w%d" % (t + 1)
-            g.wait_ge(T.sem["h" + k], on_chip(1))
-            n += fwd(dests[t + 1], T["b" + k][:, :], T["h" + k][:, :], "r" + k)
+        for m, h in (("w", 0), ("x", 2)):
+            if t < 2 and core == _helpers(rc, dests[t + 1], topo)[h]:
+                k = "%s%d" % (m, t + 1)
+                g.wait_ge(T.sem["h" + k], on_chip(1))
+                n += fwd(dests[t + 1], T["b" + k][:, :], T["h" + k][:, :], "r" + k)
         for h, lo, sem in ((a, 0, "rqa"), (b, C // 2, "rqb")):
             if core == h:
                 k = "q%d" % t
@@ -84,10 +84,6 @@ def _relay(g, core, rc, T, topo):
             k = "s%d" % t
             g.wait_ge(T.sem["h" + k], on_chip(1))
             n += fwd(dest, T["r" + k][:, :], T["h" + k][:, :], "r" + k)
-        if t < 2 and core == _helpers(rc, dests[t + 1], topo)[2]:
-            k = "x%d" % (t + 1)
-            g.wait_ge(T.sem["h" + k], on_chip(1))
-            n += fwd(dests[t + 1], T["b" + k][:, :], T["h" + k][:, :], "r" + k)
     if n: g.wait_ge(T.sem["sent"], n)
 
 
@@ -131,7 +127,7 @@ def rank_program(g, core, T, topo):
     def arrived(regions, *events):
         for r in regions: last_write[r], readers[r] = [(s, n, {}) for s, n in events], []
 
-    def load(q, dst, src, sem, writes): call(q, lambda e: e.dma_start(dst, src), [], writes, sem, 16)
+    def load(q, dst, src, sem, writes, after=()): call(q, lambda e: e.dma_start(dst, src), list(after), writes, sem, 16)
 
     def store(q, dst, src, reads): call(q, lambda e: e.dma_start(dst, src), reads, [], "store", 16)
 
@@ -141,11 +137,11 @@ def rank_program(g, core, T, topo):
         if op1 is None: call("v", lambda e: e.tensor_scalar(out, in0, s1, None, op0), reads, writes)
         else: call("v", lambda e: e.tensor_scalar(out, in0, s1, s2, op0, op1), reads, writes)
 
-    def vcopy(out, in_, reads, writes): call("v", lambda e: e.tensor_copy(out, in_), reads, writes)
-
-    def scopy(out, in_, reads, writes, scale=1.0):
-        if scale == 1.0: call("s", lambda e: e.activation(out, in_, COPY), reads, writes)
-        else: call("s", lambda e: e.activation(out, in_, COPY, scale=scale), reads, writes)
+    def copy(q, out, in_, reads, writes, scale=1.0):
+        if q == "s" and scale == 1.0: call("s", lambda e: e.activation(out, in_, COPY), reads, writes)
+        elif q == "s": call("s", lambda e: e.activation(out, in_, COPY, scale=scale), reads, writes)
+        elif scale == 1.0: call("v", lambda e: e.tensor_copy(out, in_), reads, writes)
+        else: ts(out, in_, scale, None, A.mult, None, reads, writes)
 
     def scan(out, d0, d1, op0, op1, reads, writes): call("v", lambda e: e.tensor_tensor_scan(out, d0, d1, 0.0, op0, op1), reads, writes)
 
@@ -153,37 +149,38 @@ def rank_program(g, core, T, topo):
 
     def mm(out, lq, ls, rq, rs, reads, writes): call("t", lambda e: e.matmul_mx(out, lq, ls, rq, rs, True, True), reads, writes)
 
-    sent = [0]
+    sent = {"sent": 0, "sod": 0}
     dests = [T.cores[rank ^ s] for s in STEP]
     back = [[len(topo.engines(h, core)) for h in _helpers(d, core, topo)] for d in dests]
 
-    def send(reads, *parts):
+    def send(reads, *parts, left="sent"):
         settle("g", [e for r in reads for e in last_write.get(r, [])])
         if len(parts) == 1:
             h, dst, src, sem, es = parts[0]
             rid, pid = topo.addr(h, core)
-            g.remote_dma(out_ap=dst, in_ap=src, remote_sem=T.sem[sem], local_sem=T.sem["sent"], pid=pid, routing_id=rid, dma_engine_mask=_mask(es))
+            g.remote_dma(out_ap=dst, in_ap=src, remote_sem=T.sem[sem], local_sem=T.sem[left], pid=pid, routing_id=rid, dma_engine_mask=_mask(es))
         else:
             moves = []
             for h, dst, src, sem, es in parts:
                 rid, pid = topo.addr(h, core)
                 moves.append(RemoteDMATransfer(dst_ids=[DstId(rid=rid, pnc=pid)], dma_engine_mask=_mask(es), remote_sem=T.sem[sem], src=src, dst=dst))
-            g.remote_dma_fused(moves, local_sem=T.sem["sent"])
-        sent[0] += sum(len(p[4]) for p in parts)
+            g.remote_dma_fused(moves, local_sem=T.sem[left])
+        sent[left] += sum(len(p[4]) for p in parts)
 
     load("y", T["odi"][:, :], T.od[:, :], "lod", ["odi"])
-    load("s", T["xin"][:, :], T.x[:, :], "lx", ["xin"])
+    load("y", T["xin"][:, :], T.x[:, :], "lx", ["xin"])
     load("y", T["uin"][:, :], T.u[:, :], "lu", ["uin"])
-    load("y", T["wq"][:, :].bitcast(dt.uint8), T.wc[:, :], "lwc", ["wq"])
-    load("y", T["wp"][:, :], T.ws[:, :], "lws", ["wp"])
-    load("y", T["vin"][:, :], T.v[:, :], "lv", ["vin"])
     ha, hb, hc = _helpers(core, dests[0], topo)
     es = topo.engines(core, ha)
     iot, ci = T["iot"], T["ci"]
-    call("g", lambda e: e.iota(iot[:, :], [[1, 512]], 0, 0, allow_small_or_imprecise_dtypes=True), [], ["iot"])
+    call("v", lambda e: e.memset(T["et"][:, :], 0.0), [], ["et"])
     call("g", lambda e: e.iota(T["pidx"][:, :], [[1, 1]], 0, 1), [], ["pidx"])
-    call("g", lambda e: e.iota(T["p4"][:, :], [[1, 4]], 0, 4, allow_small_or_imprecise_dtypes=True), [], ["p4"])
-    send(["odi"], (ha, T["hod"][:, :], T["odi"][:, :], "hod", es[1::2]))
+    call("g", lambda e: e.iota(iot[:, :], [[1, C]], 0, 0, allow_small_or_imprecise_dtypes=True), [], ["iot"])
+    send(["odi"], (ha, T["hod"][:, :], T["odi"][:, :], "hod", es[1::2]), left="sod")
+    arrived(["od gone"], ("sod", sent["sod"]))
+    load("y", T["wq"][:, :].bitcast(dt.uint8), T.wc[:, :], "lwc", ["wq"], ["od gone"])
+    load("y", T["wp"][:, :], T.ws[:, :], "lws", ["wp"])
+    load("y", T["vin"][:, :], T.v[:, :], "lv", ["vin"])
     arrived(["bi"], ("roda", back[0][0]))
     arrived(["bv"], ("rivb", back[0][1]), ("rivc", back[0][2]))
     for t in range(3):
@@ -192,33 +189,25 @@ def rank_program(g, core, T, topo):
             arrived(["bx%d" % t], ("rx%d" % t, back[t][2]))
         arrived(["rz%d" % t], ("rqa%d" % t, back[t][0]), ("rqb%d" % t, back[t][1]), ("rs%d" % t, back[t][2]))
 
-    ts(ci[:, :], iot[:, 0:C], -144.0, None, A.add, None, ["iot"], ["ci"])
     ts(T["p15"][:, :], T["pidx"][:, :], 15, None, A.bitwise_and, None, ["pidx"], ["p15"])
-    vcopy(T["p16"][:, :], T["p15"][:, :], ["p15"], ["p16"])
-    ts(T["ofc"][:, :], iot[:, 0:36], 0.0, T["p16"][:, :], A.mult, A.add, ["iot", "p16"], ["ofc"])
-    ts(T["ne"][:, :], iot[:, 0:16], T["p16"][:, :], None, A.not_equal, None, ["iot", "p16"], ["ne"])
+    copy("v", T["p1"][:, :], T["pidx"][:, :], ["pidx"], ["p1"])
+    copy("v", T["p16"][:, :], T["p15"][:, :], ["p15"], ["p16"])
     ts(T["nx"][:, :], iot[:, 0:16], T["p16"][:, :], 1.0, A.subtract, A.is_equal, ["iot", "p16"], ["nx"])
+    ts(T["ne"][:, :], iot[:, 0:16], T["p16"][:, :], None, A.not_equal, None, ["iot", "p16"], ["ne"])
     ts(T["t1"][:, :], T["nx"][:, :], 1048575.0, None, A.mult, None, ["nx"], ["t1"])
+    ts(T["ofc"][:, :], iot[:, 0:18], 0.0, T["p16"][:, :], A.mult, A.add, ["iot", "p16"], ["ofc"])
     tt(T["sc16"][:, :], T["t1"][:, :], T["ne"][:, :], A.add, ["t1", "ne"], ["sc16"])
     ts(T["sct"][:, :], T["p16"][:, :], 15.0, 1.0 - 2.0 ** -20, A.is_equal, A.mult, ["p16"], ["sct"])
+    ts(ci[:, :], iot[:, :], -144.0, None, A.add, None, ["iot"], ["ci"])
     ts(T["scol"][:, :], T["sct"][:, :], 2.0 ** -20, None, A.add, None, ["sct"], ["scol"])
-    scopy(T["scc"][:, :], T["sc16"][:, :].indirect(T["ofc"][:, :]), ["sc16", "ofc"], ["scc"])
+    copy("s", T["scc"][:, :], T["sc16"][:, :].indirect(T["ofc"][:, :]), ["sc16", "ofc"], ["scc"])
 
-    def wrap(src, out, writes):
-        scan(T["zj"][:, :], T["scc"][:, 0:C], T[src][:, :], A.mult, A.add, ["scc", src], ["zj"])
-        ts(out, T["zj"][:, 15:C:16], T["scol"][:, :], 144.25, A.mult, A.add, ["zj", "scol"], writes)
-
-    vcopy(T["aw0"][:, 18:36], T["odi"][:, :], ["odi"], ["aw0.o"])
-    vcopy(T["ivr"][:, :].indirect(T["aw0"][:, 18:36]), ci[:, :], ["ci", "aw0.o"], ["ivr"])
-    wrap("ivr", T["aw0"][:, 0:18], ["aw0.i"])
-    vcopy(T["ivi"][:, :], T["aw0"][:, 0:18], ["aw0.i"], ["ivi"])
-    send(["ivi"], (hb, T["hiv"][:, 0:9], T["ivi"][:, 0:9], "hiv", es[0::4]), (hc, T["hiv"][:, 9:18], T["ivi"][:, 9:18], "hiv", es[2::4]))
+    def wrap(src, out, writes, z="zj"):
+        scan(T[z][:, :], T["scc"][:, :], T[src][:, :], A.mult, A.add, ["scc", src], [z])
+        ts(out, T[z][:, 15:C:16], T["scol"][:, :], 144.25, A.mult, A.add, [z, "scol"], writes)
 
     def off(t, k):
-        return T["aw%d" % t][:, 0:18] if k == "i" else T["aw%d" % t][:, 18:36]
-
-    def keys(t):
-        tt(T["k0"][:, :], T["i5"][:, :].indirect(off(t, "i")), iot[:, 0:C], A.add, ["i5", "aw%d.i" % t, "iot"], ["k0"])
+        return T["aw%d" % t][:, 0:18] if k == "o" else T["aw%d" % t][:, 18:36]
 
     def bank(p, b, n=C): return T[p][:, 512 * b:512 * b + n]
 
@@ -232,110 +221,92 @@ def rank_program(g, core, T, topo):
         q, s = T["xq%d" % t], T["xs%d" % t]
         mm(bank("pd", b), T["eq"][:, 128 * b:128 * b + 128], T["ep"][:, 128 * b:128 * b + 128], q[:, :], s[:, :], ["e", "x%d" % t], ["pd%d" % b])
 
-    def held(b): scopy(part("fs", b), bank("pd", b), ["pd%d" % b], ["fs%d" % b])
+    def held(q, b): copy(q, part("fs", b), bank("pd", b), ["pd%d" % b], ["fs%d" % b])
 
-    def signs(): call("s", lambda e: e.activation(T["fl"][:, :], bank("pr", 0), SIGN), ["pr0"], ["fl"])
+    def signs(t):
+        call("s", lambda e: e.activation(T["fl"][:, :], bank("pr", 0), SIGN), ["pr0"], ["fl"])
+        call("s", lambda e: e.activation(T["flp"][:, :], T["fl"][:, :].indirect(off(t, "o")), RELU), ["fl", "aw%d.o" % t], ["flp"])
 
     def shifted(out, in_, reads, writes): ts(out, in_, 0.25, None, A.add, None, reads, writes)
 
-    def chase(t, mid):
+    def others(t, h):
+        src = (("bi", "bv")[h] if t == 0 else ("bw%d", "bx%d")[h] % t)
+        k, a, b = str(h), 18 * h, 18 * h + 18
+        return [lambda: shifted(T["bf"][:, a:b], T[src][:, :], [src], ["bf" + k]),
+                lambda: tt(T["df"][:, a:b], T["bf"][:, a:b], T["af%d" % t][:, a:b], A.subtract, ["bf" + k, "af%d.%d" % (t, h)], ["df" + k]),
+                lambda: ts(T["ds"][:, a:b], T["df"][:, a:b], T["scol"][:, :], None, A.mult, None, ["df" + k, "scol"], ["ds" + k])]
+
+    def own(t, h): shifted(T["af%d" % t][:, 18 * h:18 * h + 18], off(t, "oi"[h]), ["aw%d.%s" % (t, "oi"[h])], ["af%d.%d" % (t, h)])
+
+    def chase(t, beside):
+        def at(i, spot):
+            for f in beside.get((i, spot), []): f()
         if t == 0:
-            vcopy(T["b0"][:, :], T["bi"][:, :], ["bi"], ["b0"])
-            scopy(T["jb"][:, :], ci[:, :].indirect(T["b0"][:, :]), ["ci", "b0"], ["jb"])
-            scopy(T["ja"][:, :], T["jb"][:, :].indirect(off(0, "i")), ["jb", "aw0.i"], ["ja"])
+            copy("v", T["b0"][:, :], T["bi"][:, :], ["bi"], ["b0"])
+            copy("s", T["ja"][:, :], T["iw0"][:, :].indirect(T["b0"][:, :]), ["iw0", "b0"], ["ja"])
         else:
-            scopy(T["ja"][:, :], T["op%d" % t][:, :].indirect(T["bw%d" % t][:, 0:18]), ["op%d" % t, "bw%d" % t], ["ja"])
-        scopy(T["c0"][:, :], T["k0"][:, :], ["k0"], ["c0"])
+            copy("s", T["ja"][:, :], T["iw%d" % t][:, :].indirect(T["bw%d" % t][:, :]), ["iw%d" % t, "bw%d" % t], ["ja"])
         wrap("ja", T["lo0"][:, :], ["lo0"])
-        jr, key, twin = "ja", "k0", "c0"
+        jr, key, twin = "ja", "ci", None
         for i, r in enumerate(RAD):
             last = i == len(RAD) - 1
             lo = "lo%d" % i
+            src = jr
             if not last:
-                src = jr
                 for m in range(r - 1):
                     dst = [x for x in ("ja", "jb", "jc") if x not in (src, jr)][0]
-                    scopy(T[dst][:, :], T[src][:, :].indirect(T[lo][:, :]), [src, lo], [dst])
+                    copy("s", T[dst][:, :], T[src][:, :].indirect(T[lo][:, :]), [src, lo], [dst])
                     src = dst
+            at(i, "step")
             acc = key
             for m in range(r - 1):
-                if last and m == r - 2: name, out = "kk0", T["kk"][:, 0:C]
-                else:
-                    name = [x for x in ("k0", "k1", "k2") if x not in (acc, key)][0]
-                    out = T[name][:, :]
-                tt(out, T[acc][:, :].indirect(T[lo][:, :]), T[twin][:, :], A.min, [acc, twin, lo], [name])
+                name = [x for x in ("k0", "k1", "k2") if x not in (acc, key)][0]
+                if twin is None: tt(T[name][:, :], T[jr][:, :], T[key][:, :], A.min, [jr, key], [name])
+                else: tt(T[name][:, :], T[acc][:, :].indirect(T[lo][:, :]), T[twin if m == 0 else key][:, :], A.min, [acc, twin if m == 0 else key, lo], [name])
                 acc = name
-                if last and m == 0: mid()
+                at(i, "min%d" % m)
             key = acc
-            if not last:
-                twin = "c1" if twin == "c0" else "c0"
-                scopy(T[twin][:, :], T[key][:, :], [key], [twin])
-                jr = src
-                wrap(jr, T["lo%d" % (i + 1)][:, :], ["lo%d" % (i + 1)])
+            if last: break
+            twin = "c1" if twin == "c0" else "c0"
+            q = beside.get((i, "twin"), "s")
+            if q == "s": copy("s", T[twin][:, :], T[key][:, :], [key], [twin])
+            jr = src
+            scan(T["zj"][:, :], T["scc"][:, :], T[jr][:, :], A.mult, A.add, ["scc", jr], ["zj"])
+            if q == "v": copy("v", T[twin][:, :], T[key][:, :], [key], [twin])
+            at(i, "scan")
+            ts(T["lo%d" % (i + 1)][:, :], T["zj"][:, 15:C:16], T["scol"][:, :], 144.25, A.mult, A.add, ["zj", "scol"], ["lo%d" % (i + 1)])
+            at(i, "off")
+        wrap(key, T["ll"][:, :], ["ll"], "zk")
 
-    def spread(h):
-        k, a, b = str(h), C * h, C * h + C
-        scan(T["zk"][:, a:b], T["dkk"][:, a:b], T["kk"][:, a:b], A.add, A.max, ["dkk", "kk" + k], ["zk" + k])
+    def take(t, h):
+        n, k, a, b = t + 1, str(h), 18 * h, 18 * h + 18
+        return [lambda: scan(T["zf" + k][:, :], T["scc"][:, :], T["tf" + k][:, :], A.mult, A.add, ["scc", "tf" + k], ["zf" + k]),
+                lambda: tt(T["fm"][:, a:b], T["zf" + k][:, 15:C:16], T["ds"][:, a:b], A.mult, ["zf" + k, "ds" + k], ["fm" + k]),
+                lambda: tt(T["fw"][:, a:b], T["fm"][:, a:b], T["af%d" % t][:, a:b], A.add, ["fm" + k, "af%d.%d" % (t, h)], ["fw" + k]),
+                lambda: copy("v", off(n, "oi"[h]), T["fw"][:, a:b], ["fw" + k], ["aw%d.%s" % (n, "oi"[h])])]
 
     def choose(t):
         n = t + 1
-        af, aw = "af%d" % t, "aw%d" % n
-
-        def leaders(h):
-            k = str(h)
-            a, b = 18 * h, 18 * h + 18
-            vcopy(T["zki"][:, a:b], T["zk"][:, C * h + 15:C * h + C:16], ["zk" + k], ["zki" + k])
-            ts(T["zkm"][:, a:b], T["zki"][:, a:b], 511, None, A.bitwise_and, None, ["zki" + k], ["zkm" + k])
-            vcopy(T["ll"][:, a:b], T["zkm"][:, a:b], ["zkm" + k], ["ll" + k])
-
-        def flags(h):
-            k = str(h)
-            call("s", lambda e: e.activation(T["tf"][:, C * h:C * h + C], T["fl"][:, :].indirect(T["ll"][:, 18 * h:18 * h + 18]), RELU), ["fl", "ll" + k], ["tf" + k])
-
-        def take(h):
-            k, r = str(h), aw + (".i", ".o")[h]
-            a, b = C * h, C * h + C
-            scan(T["zf"][:, a:b], T["scc"][:, a:b], T["tf"][:, a:b], A.mult, A.add, ["scc", "tf" + k], ["zf" + k])
-            a, b = 18 * h, 18 * h + 18
-            tt(T["fm"][:, a:b], T["zf"][:, C * h + 15:C * h + C:16], T["ds"][:, a:b], A.mult, ["zf" + k, "ds"], ["fm" + k])
-            tt(T["fw"][:, a:b], T["fm"][:, a:b], T[af][:, a:b], A.add, ["fm" + k, af], ["fw" + k])
-            vcopy(T[aw][:, a:b], T["fw"][:, a:b], ["fw" + k], [r])
-        scopy(T["kk"][:, C:2 * C], T["kk"][:, 0:C].indirect(off(t, "o")), ["kk0", "aw%d.o" % t], ["kk1"])
-        leaders(0)
-        signs()
-        if t == 0:
-            shifted(T["bf"][:, 0:18], T["bv"][:, :], ["bv"], ["bf.i"])
-            shifted(T["bf"][:, 18:36], T["bi"][:, :], ["bi"], ["bf.o"])
-        else:
-            shifted(T["bf"][:, 0:18], T["bw%d" % t][:, :], ["bw%d" % t], ["bf.i"])
-            shifted(T["bf"][:, 18:36], T["bx%d" % t][:, :], ["bx%d" % t], ["bf.o"])
-        tt(T["df"][:, :], T["bf"][:, :], T[af][:, :], A.subtract, ["bf.i", "bf.o", af], ["df"])
-        ts(T["ds"][:, :], T["df"][:, :], T["scol"][:, :], None, A.mult, None, ["df", "scol"], ["ds"])
-        flags(0)
-        spread(1)
-        leaders(1)
-        if t: held(0)
-        flags(1)
-        take(0)
-        if n < 3: send([aw + ".i"], (_helpers(core, dests[n], topo)[0], T["hw%d" % n][:, :], T[aw][:, 0:18], "hw%d" % n, es))
-        take(1)
-        if t:
-            for b in (1, 2): held(b)
+        copy("s", T["tf0"][:, :], T["flp"][:, :].indirect(T["ll"][:, :]), ["flp", "ll"], ["tf0"])
+        copy("s", T["tf1"][:, :], T["tf0"][:, :].indirect(off(t, "i")), ["tf0", "aw%d.i" % t], ["tf1"])
+        for f in take(t, 0): f()
+        if n < 3: send(["aw%d.o" % n], (_helpers(core, dests[n], topo)[0], T["hw%d" % n][:, :], off(n, "o"), "hw%d" % n, es))
 
     def means(t):
         n = t + 1
-        o, ro = off(n, "o"), "aw%d.o" % n
+        o, ro, ri = off(n, "o"), "aw%d.o" % n, "aw%d.i" % n
+        places = take(t, 1)
 
-        def pair(b): tt(part("ys", b), part("gs", b), bank("pd", b), A.add, ["gs%d" % b, "pd%d" % b], ["ys%d" % b])
-        for b in (1, 2, 3):
-            scopy(part("gs", b), part("fs", b).indirect(o), ["fs%d" % b, ro], ["gs%d" % b])
-            if t and b == 1: held(3)
-        vcopy(part("gs", 0), part("fs", 0).indirect(o), ["fs0", ro], ["gs0"])
-        for k, b in ("y1", "y0", "z1", "y2", "y3", "z2"):
-            b = int(b)
-            if k == "y": pair(b)
-            else: ts(T["zt"][:, b:4 * C:4], part("ys", b).indirect(o), 0.5, None, A.mult, None, ["ys%d" % b, ro], ["zt%d" % b])
-        for b in (0, 3): scopy(T["zt"][:, b:4 * C:4], part("ys", b).indirect(o), ["ys%d" % b, ro], ["zt%d" % b], 0.5)
+        def g_(q, b): copy(q, part("gs", b), part("fs", b).indirect(o), ["fs%d" % b, ro], ["gs%d" % b])
+
+        def y_(b): tt(part("ys", b), part("gs", b), bank("pd", b), A.add, ["gs%d" % b, "pd%d" % b], ["ys%d" % b])
+
+        def z_(q, b): copy(q, T["zt"][:, b:4 * C:4], part("ys", b).indirect(o), ["ys%d" % b, ro], ["zt%d" % b], 2.0 ** -6)
+        g_("v", 0); g_("s", 1); g_("s", 2); g_("s", 3)
+        places[0](); y_(0); places[1](); y_(1); places[2](); y_(2); places[3]()
+        if n < 3: send([ri], (_helpers(core, dests[n], topo)[2], T["hx%d" % n][:, :], off(n, "i"), "hx%d" % n, es))
+        z_("s", 0); y_(3); z_("v", 1); z_("s", 2); z_("v", 3)
+        if n < 3: copy("s", T["iw%d" % n][:, :], ci[:, :].indirect(off(n, "i")), ["ci", ri], ["iw%d" % n])
         zq, zs = T["zq%d" % t], T["zs%d" % t]
         quant(zq[:, :], zs[:, :], T["zt"][:, :], ["zt0", "zt1", "zt2", "zt3"], ["z%d" % t])
         a, b, c = _helpers(core, dests[t], topo)
@@ -344,74 +315,74 @@ def rank_program(g, core, T, topo):
              (b, hq[:, h:C].bitcast(dt.uint8), zq[:, h:C].bitcast(dt.uint8), "hq%d" % t, es[0::2]))
         send(["z%d" % t], (c, T["hs%d" % t][:, :], zs[:, :], "hs%d" % t, es))
         if n < 3:
-            send([ro], (_helpers(core, dests[n], topo)[2], T["hx%d" % n][:, :], o, "hx%d" % n, es))
-            scopy(T["op%d" % n][:, :], ci[:, :].indirect(o), ["ci", ro], ["op%d" % n])
-            keys(n)
-            shifted(T["af%d" % n][:, :], T["aw%d" % n][:, :], ["aw%d.i" % n, "aw%d.o" % n], ["af%d" % n])
-        for b in SUMMED: scopy(part("fp", b), part("fs", b).indirect(o), ["fs%d" % b, ro], ["fp%d" % b], 32.0)
+            for h in (0, 1): own(n, h)
 
-    def products(t):
-        n = t + 1
-        i, ri = off(n, "i"), "aw%d.i" % n
+    def layer(t):
         rq, rs = T["rq%d" % t], T["rs%d" % t]
         for b in range(4):
             mm(bank("pr", b), T["wq"][:, 128 * b:128 * b + 128], T["wp"][:, 128 * b:128 * b + 128], rq[:, :], rs[:, :], ["wq", "wp", "rz%d" % t], ["pr%d" % b])
-        for b in SUMMED: tt(part("rr", b), bank("pr", b), part("fp", b), A.add, ["pr%d" % b, "fp%d" % b], ["rr%d" % b])
 
-        def scaled(b): scopy(part("rr", b), bank("pr", b), ["pr%d" % b], ["rr%d" % b], 0.03125)
+    def summed(b): tt(part("rr", b), bank("pr", b), part("gs", b), A.add, ["pr%d" % b, "gs%d" % b], ["rr%d" % b])
 
-        def moved(b): scopy(T["xt"][:, b:4 * C:4], part("rr", b).indirect(i), ["rr%d" % b, ri], ["xt%d" % b], 0.03125)
-        for f, b in ((scaled, 1), (moved, 0), (scaled, 3), (moved, 2)): f(b)
+    def moved(t, q, b): copy(q, T["xt"][:, b:4 * C:4], part("rr", b).indirect(off(t + 1, "i")), ["rr%d" % b, "aw%d.i" % (t + 1)], ["xt%d" % b], 2.0 ** -5)
 
-    def state(t):
-        n = t + 1
-        i, ri = off(n, "i"), "aw%d.i" % n
-        for b in range(4):
-            if b not in SUMMED: tt(T["xt"][:, b:4 * C:4], part("rr", b).indirect(i), part("fs", b), A.add, ["rr%d" % b, ri, "fs%d" % b], ["xt%d" % b])
-        if n < 3: spread(0)
+    def state(n):
         quant(T["xq%d" % n][:, :], T["xs%d" % n][:, :], T["xt"][:, :], ["xt0", "xt1", "xt2", "xt3"], ["x%d" % n])
         if n < 3:
             score(n)
             for b in range(4): unpack(n, b)
 
-    ts(T["t1"][:, :], T["ne"][:, :], 1.0, 2.0 ** 20, A.subtract, A.mult, ["ne"], ["t1"])
-    ts(T["t2"][:, :], T["nx"][:, :], 2.0 ** 18, None, A.mult, None, ["nx"], ["t2"])
-    tt(T["dk16"][:, :], T["t1"][:, :], T["t2"][:, :], A.add, ["t1", "t2"], ["dk16"])
-    scopy(T["dkk"][:, :], T["dk16"][:, :].indirect(T["ofc"][:, :]), ["dk16", "ofc"], ["dkk"])
-    ts(T["i5"][:, :], iot[:, 0:C], 512.0, None, A.mult, None, ["iot"], ["i5"])
-    keys(0)
+    for b in range(4): ts(T["et"][:, 512 * b + b:512 * b + 512:4], iot[:, 0:128], T["p1"][:, :], 32.0, A.is_equal, A.mult, ["iot", "p1", "et"], ["et%d" % b])
     ts(T["uof"][:, :], iot[:, 0:8], 16.0, None, A.mult, None, ["iot"], ["uof"])
-    for b in range(4): ts(T["et"][:, 512 * b:512 * b + 512], iot[:, :], T["p4"][:, b:b + 1], None, A.is_equal, None, ["iot", "p4"], ["et%d" % b])
+    copy("v", off(0, "o"), T["odi"][:, :], ["odi"], ["aw0.o"])
+    copy("v", T["iw0"][:, :].indirect(off(0, "o")), ci[:, :], ["ci", "aw0.o"], ["iw0"])
+    wrap("iw0", off(0, "i"), ["aw0.i"])
+    copy("v", T["ivi"][:, :], off(0, "i"), ["aw0.i"], ["ivi"])
+    send(["ivi"], (hb, T["hiv"][:, 0:9], T["ivi"][:, 0:9], "hiv", es[0::4]), (hc, T["hiv"][:, 9:18], T["ivi"][:, 9:18], "hiv", es[2::4]))
     quant(T["eq"][:, :], T["ep"][:, :], T["et"][:, :], ["et0", "et1", "et2", "et3"], ["e"])
     quant(T["xq0"][:, :], T["xs0"][:, :], T["xin"][:, :], ["xin"], ["x0"])
     for b in range(4): unpack(0, b)
-    for b in range(4): held(b)
+    for b in range(4): held("s", b)
     quant(T["uq"][:, :], T["up"][:, :], T["uin"][:, :], ["uin"], ["u"])
-    vcopy(T["urq"][:, :].bitcast(dt.uint32), T["uq"][:, :].bitcast(dt.uint32).indirect(T["uof"][:, :]), ["u", "uof"], ["urq"])
-    vcopy(T["urp"][:, :], T["up"][:, :].indirect(T["uof"][:, :]), ["u", "uof"], ["urp"])
+    copy("v", T["urq"][:, :].bitcast(dt.uint32), T["uq"][:, :].bitcast(dt.uint32).indirect(T["uof"][:, :]), ["u", "uof"], ["urq"])
+    copy("v", T["urp"][:, :], T["up"][:, :].indirect(T["uof"][:, :]), ["u", "uof"], ["urp"])
     score(0)
-    shifted(T["af0"][:, :], T["aw0"][:, :], ["aw0.i", "aw0.o"], ["af0"])
-    chase(0, lambda: None)
-    spread(0)
+    signs(0)
+    for h in (0, 1): own(0, h)
+
+    def small(t):
+        calls = others(t, 0) + others(t, 1)
+        return {(k, "scan"): [calls[k]] for k in range(6)}
+    chase(0, small(0))
     choose(0)
     means(0)
     for t in (1, 2):
-        chase(t, lambda: products(t - 1))
-        state(t - 1)
+        p = t - 1
+        plan = small(t)
+        plan[(5, "step")] = [lambda: layer(p)]
+        plan[(5, "min1")] = [lambda: summed(0)]
+        plan[(5, "twin")] = "v"
+        plan[(5, "off")] = [lambda: summed(1), lambda: moved(p, "s", 0), lambda: moved(p, "s", 1)]
+        plan[(6, "min0")] = [lambda: summed(2), lambda: summed(3), lambda: moved(p, "s", 2)]
+        plan[(6, "min1")] = [lambda: moved(p, "v", 3), lambda: state(t), lambda: signs(t)]
+        chase(t, plan)
+        for b in range(4): held("v", b)
         choose(t)
         means(t)
     quant(T["vq"][:, :], T["vp"][:, :], T["vin"][:, :], ["vin"], ["v"])
-    vcopy(T["fr"][:, :], iot[:, 0:C].indirect(off(3, "o")), ["iot", "aw3.o"], ["fr"])
+    copy("s", T["fr"][:, :], iot[:, :].indirect(off(3, "o")), ["iot", "aw3.o"], ["fr"])
     for k in range(8): store("y", T.fo[k:k + 1, :], T["fr"][16 * k:16 * k + 1, :], ["fr"])
-    products(2)
-    state(2)
+    layer(2)
+    for b in range(4): summed(b)
+    for q, b in (("s", 0), ("s", 1), ("s", 2), ("v", 3)): moved(2, q, b)
+    state(3)
     store("y", T.oc[:, :], T["xq3"][:, :].bitcast(dt.uint8), ["x3"])
     h = C // 2
     for k in range(2): mm(bank("pr", k, h), T["vq"][:, :], T["vp"][:, :], T["xq3"][:, h * k:h * k + h], T["xs3"][:, h * k:h * k + h], ["v", "x3"], ["pr%d" % k])
     for k in range(4): store("y" if k < 2 else "s", T.osc[4 * k:4 * k + 4, :], T["xs3"][32 * k:32 * k + 4, :], ["x3"])
-    vcopy(T["yo"][:, 0:h], bank("pr", 0, h), ["pr0"], ["yo0"])
-    scopy(T["yo"][:, h:C], bank("pr", 1, h), ["pr1"], ["yo1"])
+    copy("v", T["yo"][:, 0:h], bank("pr", 0, h), ["pr0"], ["yo0"])
+    copy("s", T["yo"][:, h:C], bank("pr", 1, h), ["pr1"], ["yo1"])
     store("y", T.y[:, 0:h], T["yo"][:, 0:h], ["yo0"])
     store("s", T.y[:, h:C], T["yo"][:, h:C], ["yo1"])
     for s in ("cv", "cs", "ct", "cg", "store"): g.wait_ge(T.sem[s], count[s])
-    g.wait_ge(T.sem["sent"], sent[0])
+    for s in sent: g.wait_ge(T.sem[s], sent[s])

@@ -6,22 +6,30 @@ STEP = [4, 1, 2]
 RAD = [2, 2, 2, 2, 2, 3, 3]
 F32, BF, I32, U16, U8, MX = "float32", "bfloat16", "int32", "uint16", "uint8", "float8_e4m3fn_x4"
 
+FIRST = ("j0 w0 o0 j1 m1 c1s w1 o1 j2 m2 c2s w2 o2 j3 m3 c3s w3 o3 j4 m4 c4s w4 o4 j5 m5 c5s w5 o5 "
+         "j6 m6 j7 m7 c7s w6 d0 o6 m8 m9 w7 d1 o7 t0 t1 k0 k1 k2 k3")
+LATER = ("p0 g0v g1s p1 y1 y0 g3s g2s p2 y3 z0s p3 i0 y2 z1v z3v z2s j0 r0 "
+         "w0 o0 j1 m1 c1s w1 o1 j2 m2 c2s w2 o2 l0 j3 m3 c3s w3 d0 o3 j4 m4 d1 c4s w4 o4 "
+         "j5 m5 a0 c5s w5 a2 o5 a3 x0s j6 m6 a1 j7 m7 x3s x1s w6 x2v o6 q0 c7s m8 f0 m9 w7 o7 "
+         "h1v f1 h2s t0 h0v k0 k1 h3s k2 k3 t1")
+LAST = ("g0v g1s g3s g2s y1 y0 y3 z0s y2 z1v z3s z2v r0 p0 p1 p2 p3 e0 "
+        "l0 a0 a1 a2 a3 x0s x1s x2s x3v q0")
+
 
 def _scratch():
     s = {}
 
     def sb(dtype, **names):
         for k in names: s[k] = ("sbuf", [128, names[k]], dtype)
-    sb(I32, odi=18, bi=18, hod=18, ivi=18, bv=18, hiv=18, pidx=1, p15=1)
-    sb(U16, ofc=18, uof=8, b0=18, ll=18)
+    sb(I32, odi=18, b0=36, ivi=18, hiv=18, pidx=1, p15=1)
+    for k in ("odd", "hod"): s[k] = ("dram", [128, 18], I32)
+    sb(U16, ofc=18, uof=8, bu=18, lo=18 * 8, b1=36, b2=36)
     for k in range(4): sb(U16, **{"aw%d" % k: 36})
-    for k in (1, 2): sb(U16, **{a + "%d" % k: 18 for a in ("hw", "bw", "hx", "bx")})
-    for k in range(len(RAD)): sb(U16, **{"lo%d" % k: 18})
+    for k in (1, 2): sb(U16, **{a + "%d" % k: 18 for a in ("hw", "hx")})
     sb(BF, xin=4 * C, uin=512, vin=512, et=2048, zt=4 * C, xt=4 * C)
-    sb(BF, ci=C, scc=C, ja=C, jb=C, jc=C, zj=C, zk=C, k0=C, k1=C, k2=C, c0=C, c1=C, fl=C, flp=C, tf0=C, tf1=C, zf0=C, zf1=C)
-    for k in range(3): sb(BF, **{"iw%d" % k: C})
+    sb(BF, ci=C, scc=C, jj=8 * C, kk=10 * C, cc=8 * C, zj=2 * C, fl=C, flp=C, tf=2 * C, zf=2 * C, iw=C)
     sb(F32, iot=C, p1=1, p16=1, sct=1, scol=1, ne=16, nx=16, t1=16, sc16=16)
-    sb(F32, gs=4 * C, bf=36, df=36, ds=36, fw=36, fm=36, af0=36, af1=36, af2=36)
+    sb(F32, gs=4 * C, bf=36, df=36, fm=36, af0=36, af1=36, af2=36, af3=36)
     sb(F32, fs=4 * C, ys=4 * C, rr=4 * C, yo=C, fr=C)
     for k, n in (("w", 512), ("e", 512), ("u", 128), ("ur", 128), ("v", 128)): sb(MX, **{k + "q": n}); sb(U8, **{k + "p": n})
     for k in range(4): sb(MX, **{"xq%d" % k: C}); sb(U8, **{"xs%d" % k: C})
@@ -33,7 +41,7 @@ def _scratch():
 
 
 SCRATCH = _scratch()
-SEMAPHORES = ["cv", "cs", "ct", "cg", "lod", "lx", "lu", "lv", "lwc", "lws", "store", "sent", "sod",
+SEMAPHORES = ["cv", "cs", "ct", "cg", "lod", "lodd", "lx", "lu", "lv", "lwc", "lws", "store", "sent", "sod", "sz",
               "hod", "hiv", "hw1", "hw2", "hx1", "hx2", "rx1", "rx2", "hq0", "hq1", "hq2", "hs0", "hs1", "hs2",
               "roda", "rivb", "rivc", "rw1", "rw2", "rqa0", "rqa1", "rqa2", "rqb0", "rqb1", "rqb2", "rs0", "rs1", "rs2"]
 
@@ -64,17 +72,17 @@ def _relay(g, core, rc, T, topo):
         a, b, c = _helpers(rc, dest, topo)
         if t == 0:
             if core == a:
-                g.wait_ge(T.sem["hod"], on_chip(2))
-                n += fwd(dest, T["bi"][:, :], T["hod"][:, :], "roda")
-            for h, lo, sem in ((b, 0, "rivb"), (c, 9, "rivc")):
+                g.wait_ge(T.sem["hod"], on_chip(4))
+                n += fwd(dest, T["b0"][:, 0:18], T["hod"][:, :], "roda")
+            for h, lo, sem, k in ((b, 0, "rivb", 2), (c, 9, "rivc", 4)):
                 if core == h:
-                    g.wait_ge(T.sem["hiv"], on_chip(4))
-                    n += fwd(dest, T["bv"][:, lo:lo + 9], T["hiv"][:, lo:lo + 9], sem)
-        for m, h in (("w", 0), ("x", 2)):
+                    g.wait_ge(T.sem["hiv"], on_chip(k))
+                    n += fwd(dest, T["b0"][:, 18 + lo:27 + lo], T["hiv"][:, lo:lo + 9], sem)
+        for m, h, lo in (("w", 0, 0), ("x", 2, 18)):
             if t < 2 and core == _helpers(rc, dests[t + 1], topo)[h]:
                 k = "%s%d" % (m, t + 1)
                 g.wait_ge(T.sem["h" + k], on_chip(1))
-                n += fwd(dests[t + 1], T["b" + k][:, :], T["h" + k][:, :], "r" + k)
+                n += fwd(dests[t + 1], T["b%d" % (t + 1)][:, lo:lo + 18], T["h" + k][:, :], "r" + k)
         for h, lo, sem in ((a, 0, "rqa"), (b, C // 2, "rqb")):
             if core == h:
                 k = "q%d" % t
@@ -143,13 +151,13 @@ def rank_program(g, core, T, topo):
         elif scale == 1.0: call("v", lambda e: e.tensor_copy(out, in_), reads, writes)
         else: ts(out, in_, scale, None, A.mult, None, reads, writes)
 
-    def scan(out, d0, d1, op0, op1, reads, writes): call("v", lambda e: e.tensor_tensor_scan(out, d0, d1, 0.0, op0, op1), reads, writes)
+    def scan(out, in_, reads, writes): call("v", lambda e: e.tensor_tensor_scan(out, T["scc"][:, :], in_, 0.0, A.mult, A.add), ["scc"] + reads, writes)
 
     def quant(q, s, in_, reads, writes): call("v", lambda e: e.quantize_mx(q, s, in_), reads, writes)
 
     def mm(out, lq, ls, rq, rs, reads, writes): call("t", lambda e: e.matmul_mx(out, lq, ls, rq, rs, True, True), reads, writes)
 
-    sent = {"sent": 0, "sod": 0}
+    sent = {"sent": 0, "sod": 0, "sz": 0}
     dests = [T.cores[rank ^ s] for s in STEP]
     back = [[len(topo.engines(h, core)) for h in _helpers(d, core, topo)] for d in dests]
 
@@ -167,26 +175,24 @@ def rank_program(g, core, T, topo):
             g.remote_dma_fused(moves, local_sem=T.sem[left])
         sent[left] += sum(len(p[4]) for p in parts)
 
+    load("y", T["odd"][:, :], T.od[:, :], "lodd", ["odd"])
     load("y", T["odi"][:, :], T.od[:, :], "lod", ["odi"])
-    load("y", T["xin"][:, :], T.x[:, :], "lx", ["xin"])
     load("y", T["uin"][:, :], T.u[:, :], "lu", ["uin"])
+    load("y", T["xin"][:, :], T.x[:, :], "lx", ["xin"])
     ha, hb, hc = _helpers(core, dests[0], topo)
     es = topo.engines(core, ha)
+    rest = [e for e in es if e not in es[1::4]]
     iot, ci = T["iot"], T["ci"]
     call("v", lambda e: e.memset(T["et"][:, :], 0.0), [], ["et"])
     call("g", lambda e: e.iota(T["pidx"][:, :], [[1, 1]], 0, 1), [], ["pidx"])
     call("g", lambda e: e.iota(iot[:, :], [[1, C]], 0, 0, allow_small_or_imprecise_dtypes=True), [], ["iot"])
-    send(["odi"], (ha, T["hod"][:, :], T["odi"][:, :], "hod", es[1::2]), left="sod")
-    arrived(["od gone"], ("sod", sent["sod"]))
-    load("y", T["wq"][:, :].bitcast(dt.uint8), T.wc[:, :], "lwc", ["wq"], ["od gone"])
-    load("y", T["wp"][:, :], T.ws[:, :], "lws", ["wp"])
-    load("y", T["vin"][:, :], T.v[:, :], "lv", ["vin"])
-    arrived(["bi"], ("roda", back[0][0]))
-    arrived(["bv"], ("rivb", back[0][1]), ("rivc", back[0][2]))
+    send(["odd"], (ha, T["hod"][:, :], T["odd"][:, :], "hod", es[1::4]), left="sod")
+    arrived(["b0.o"], ("roda", back[0][0]))
+    arrived(["b0.i"], ("rivb", back[0][1]), ("rivc", back[0][2]))
     for t in range(3):
         if t:
-            arrived(["bw%d" % t], ("rw%d" % t, back[t][0]))
-            arrived(["bx%d" % t], ("rx%d" % t, back[t][2]))
+            arrived(["b%d.o" % t], ("rw%d" % t, back[t][0]))
+            arrived(["b%d.i" % t], ("rx%d" % t, back[t][2]))
         arrived(["rz%d" % t], ("rqa%d" % t, back[t][0]), ("rqb%d" % t, back[t][1]), ("rs%d" % t, back[t][2]))
 
     ts(T["p15"][:, :], T["pidx"][:, :], 15, None, A.bitwise_and, None, ["pidx"], ["p15"])
@@ -202,187 +208,139 @@ def rank_program(g, core, T, topo):
     ts(T["scol"][:, :], T["sct"][:, :], 2.0 ** -20, None, A.add, None, ["sct"], ["scol"])
     copy("s", T["scc"][:, :], T["sc16"][:, :].indirect(T["ofc"][:, :]), ["sc16", "ofc"], ["scc"])
 
-    def wrap(src, out, writes, z="zj"):
-        scan(T[z][:, :], T["scc"][:, :], T[src][:, :], A.mult, A.add, ["scc", src], [z])
-        ts(out, T[z][:, 15:C:16], T["scol"][:, :], 144.25, A.mult, A.add, [z, "scol"], writes)
-
-    def off(t, k):
-        return T["aw%d" % t][:, 0:18] if k == "o" else T["aw%d" % t][:, 18:36]
+    def part(name, b, n=C): return T[name][:, n * b:n * b + n]
 
     def bank(p, b, n=C): return T[p][:, 512 * b:512 * b + n]
 
-    def part(name, b): return T[name][:, C * b:C * b + C]
+    def off(t, h): return part("aw%d" % t, h, 18)
 
-    def score(t):
-        q, s = T["xq%d" % t], T["xs%d" % t]
-        mm(bank("pr", 0), T["urq"][:, :], T["urp"][:, :], q[:, :], s[:, :], ["urq", "urp", "x%d" % t], ["pr0"])
-
-    def unpack(t, b):
-        q, s = T["xq%d" % t], T["xs%d" % t]
-        mm(bank("pd", b), T["eq"][:, 128 * b:128 * b + 128], T["ep"][:, 128 * b:128 * b + 128], q[:, :], s[:, :], ["e", "x%d" % t], ["pd%d" % b])
-
-    def held(q, b): copy(q, part("fs", b), bank("pd", b), ["pd%d" % b], ["fs%d" % b])
-
-    def signs(t):
-        call("s", lambda e: e.activation(T["fl"][:, :], bank("pr", 0), SIGN), ["pr0"], ["fl"])
-        call("s", lambda e: e.activation(T["flp"][:, :], T["fl"][:, :].indirect(off(t, "o")), RELU), ["fl", "aw%d.o" % t], ["flp"])
-
-    def shifted(out, in_, reads, writes): ts(out, in_, 0.25, None, A.add, None, reads, writes)
-
-    def others(t, h):
-        src = (("bi", "bv")[h] if t == 0 else ("bw%d", "bx%d")[h] % t)
-        k, a, b = str(h), 18 * h, 18 * h + 18
-        return [lambda: shifted(T["bf"][:, a:b], T[src][:, :], [src], ["bf" + k]),
-                lambda: tt(T["df"][:, a:b], T["bf"][:, a:b], T["af%d" % t][:, a:b], A.subtract, ["bf" + k, "af%d.%d" % (t, h)], ["df" + k]),
-                lambda: ts(T["ds"][:, a:b], T["df"][:, a:b], T["scol"][:, :], None, A.mult, None, ["df" + k, "scol"], ["ds" + k])]
-
-    def own(t, h): shifted(T["af%d" % t][:, 18 * h:18 * h + 18], off(t, "oi"[h]), ["aw%d.%s" % (t, "oi"[h])], ["af%d.%d" % (t, h)])
-
-    def chase(t, beside):
-        def at(i, spot):
-            for f in beside.get((i, spot), []): f()
-        if t == 0:
-            copy("v", T["b0"][:, :], T["bi"][:, :], ["bi"], ["b0"])
-            copy("s", T["ja"][:, :], T["iw0"][:, :].indirect(T["b0"][:, :]), ["iw0", "b0"], ["ja"])
-        else:
-            copy("s", T["ja"][:, :], T["iw%d" % t][:, :].indirect(T["bw%d" % t][:, :]), ["iw%d" % t, "bw%d" % t], ["ja"])
-        wrap("ja", T["lo0"][:, :], ["lo0"])
-        jr, key, twin = "ja", "ci", None
-        for i, r in enumerate(RAD):
-            last = i == len(RAD) - 1
-            lo = "lo%d" % i
-            src = jr
-            if not last:
-                for m in range(r - 1):
-                    dst = [x for x in ("ja", "jb", "jc") if x not in (src, jr)][0]
-                    copy("s", T[dst][:, :], T[src][:, :].indirect(T[lo][:, :]), [src, lo], [dst])
-                    src = dst
-            at(i, "step")
-            acc = key
-            for m in range(r - 1):
-                name = [x for x in ("k0", "k1", "k2") if x not in (acc, key)][0]
-                if twin is None: tt(T[name][:, :], T[jr][:, :], T[key][:, :], A.min, [jr, key], [name])
-                else: tt(T[name][:, :], T[acc][:, :].indirect(T[lo][:, :]), T[twin if m == 0 else key][:, :], A.min, [acc, twin if m == 0 else key, lo], [name])
-                acc = name
-                at(i, "min%d" % m)
-            key = acc
-            if last: break
-            twin = "c1" if twin == "c0" else "c0"
-            q = beside.get((i, "twin"), "s")
-            if q == "s": copy("s", T[twin][:, :], T[key][:, :], [key], [twin])
-            jr = src
-            scan(T["zj"][:, :], T["scc"][:, :], T[jr][:, :], A.mult, A.add, ["scc", jr], ["zj"])
-            if q == "v": copy("v", T[twin][:, :], T[key][:, :], [key], [twin])
-            at(i, "scan")
-            ts(T["lo%d" % (i + 1)][:, :], T["zj"][:, 15:C:16], T["scol"][:, :], 144.25, A.mult, A.add, ["zj", "scol"], ["lo%d" % (i + 1)])
-            at(i, "off")
-        wrap(key, T["ll"][:, :], ["ll"], "zk")
-
-    def take(t, h):
-        n, k, a, b = t + 1, str(h), 18 * h, 18 * h + 18
-        return [lambda: scan(T["zf" + k][:, :], T["scc"][:, :], T["tf" + k][:, :], A.mult, A.add, ["scc", "tf" + k], ["zf" + k]),
-                lambda: tt(T["fm"][:, a:b], T["zf" + k][:, 15:C:16], T["ds"][:, a:b], A.mult, ["zf" + k, "ds" + k], ["fm" + k]),
-                lambda: tt(T["fw"][:, a:b], T["fm"][:, a:b], T["af%d" % t][:, a:b], A.add, ["fm" + k, "af%d.%d" % (t, h)], ["fw" + k]),
-                lambda: copy("v", off(n, "oi"[h]), T["fw"][:, a:b], ["fw" + k], ["aw%d.%s" % (n, "oi"[h])])]
-
-    def choose(t):
-        n = t + 1
-        copy("s", T["tf0"][:, :], T["flp"][:, :].indirect(T["ll"][:, :]), ["flp", "ll"], ["tf0"])
-        copy("s", T["tf1"][:, :], T["tf0"][:, :].indirect(off(t, "i")), ["tf0", "aw%d.i" % t], ["tf1"])
-        for f in take(t, 0): f()
-        if n < 3: send(["aw%d.o" % n], (_helpers(core, dests[n], topo)[0], T["hw%d" % n][:, :], off(n, "o"), "hw%d" % n, es))
-
-    def means(t):
-        n = t + 1
-        o, ro, ri = off(n, "o"), "aw%d.o" % n, "aw%d.i" % n
-        places = take(t, 1)
-
-        def g_(q, b): copy(q, part("gs", b), part("fs", b).indirect(o), ["fs%d" % b, ro], ["gs%d" % b])
-
-        def y_(b): tt(part("ys", b), part("gs", b), bank("pd", b), A.add, ["gs%d" % b, "pd%d" % b], ["ys%d" % b])
-
-        def z_(q, b): copy(q, T["zt"][:, b:4 * C:4], part("ys", b).indirect(o), ["ys%d" % b, ro], ["zt%d" % b], 2.0 ** -6)
-        g_("v", 0); g_("s", 1); g_("s", 2); g_("s", 3)
-        places[0](); y_(0); places[1](); y_(1); places[2](); y_(2); places[3]()
-        if n < 3: send([ri], (_helpers(core, dests[n], topo)[2], T["hx%d" % n][:, :], off(n, "i"), "hx%d" % n, es))
-        z_("s", 0); y_(3); z_("v", 1); z_("s", 2); z_("v", 3)
-        if n < 3: copy("s", T["iw%d" % n][:, :], ci[:, :].indirect(off(n, "i")), ["ci", ri], ["iw%d" % n])
-        zq, zs = T["zq%d" % t], T["zs%d" % t]
-        quant(zq[:, :], zs[:, :], T["zt"][:, :], ["zt0", "zt1", "zt2", "zt3"], ["z%d" % t])
-        a, b, c = _helpers(core, dests[t], topo)
-        hq, h = T["hq%d" % t], C // 2
-        send(["z%d" % t], (a, hq[:, 0:h].bitcast(dt.uint8), zq[:, 0:h].bitcast(dt.uint8), "hq%d" % t, es[1::2]),
-             (b, hq[:, h:C].bitcast(dt.uint8), zq[:, h:C].bitcast(dt.uint8), "hq%d" % t, es[0::2]))
-        send(["z%d" % t], (c, T["hs%d" % t][:, :], zs[:, :], "hs%d" % t, es))
-        if n < 3:
-            for h in (0, 1): own(n, h)
-
-    def layer(t):
-        rq, rs = T["rq%d" % t], T["rs%d" % t]
-        for b in range(4):
-            mm(bank("pr", b), T["wq"][:, 128 * b:128 * b + 128], T["wp"][:, 128 * b:128 * b + 128], rq[:, :], rs[:, :], ["wq", "wp", "rz%d" % t], ["pr%d" % b])
-
-    def summed(b): tt(part("rr", b), bank("pr", b), part("gs", b), A.add, ["pr%d" % b, "gs%d" % b], ["rr%d" % b])
-
-    def moved(t, q, b): copy(q, T["xt"][:, b:4 * C:4], part("rr", b).indirect(off(t + 1, "i")), ["rr%d" % b, "aw%d.i" % (t + 1)], ["xt%d" % b], 2.0 ** -5)
+    def rounded(out, z, writes): ts(out, T["zj"][:, C * z + 15:C * z + C:16], T["scol"][:, :], 144.25, A.mult, A.add, ["zj%d" % z, "scol"], writes)
 
     def state(n):
-        quant(T["xq%d" % n][:, :], T["xs%d" % n][:, :], T["xt"][:, :], ["xt0", "xt1", "xt2", "xt3"], ["x%d" % n])
+        q, s = T["xq%d" % n], T["xs%d" % n]
+        if n: quant(q[:, :], s[:, :], T["xt"][:, :], ["xt0", "xt1", "xt2", "xt3"], ["x%d" % n])
+        else: quant(q[:, :], s[:, :], T["xin"][:, :], ["xin"], ["x0"])
         if n < 3:
-            score(n)
-            for b in range(4): unpack(n, b)
+            mm(bank("pr", 0), T["urq"][:, :], T["urp"][:, :], q[:, :], s[:, :], ["urq", "urp", "x%d" % n], ["pr0"])
+            for b in range(4): mm(bank("pd", b), part("eq", b, 128), part("ep", b, 128), q[:, :], s[:, :], ["e", "x%d" % n], ["pd%d" % b])
+
+    stage, base, wsrc = [None], [None], [0]
+    for i, r in enumerate(RAD):
+        first = len(stage) - 1
+        for m in range(r - 1): stage.append(i); base.append(first)
+        wsrc.append(len(stage) - 1)
+
+    def steps(t):
+        n, p = t + 1, t - 1
+        own, nxt = "aw%d." % t, "aw%d." % n
+
+        def lo(i): return part("lo", i, 18)
+
+        def j(k, q):
+            if k: return copy("s", part("jj", k), part("jj", k - 1).indirect(lo(stage[k])), ["jj%d" % (k - 1), "lo%d" % stage[k]], ["jj%d" % k])
+            if t: return copy("s", part("jj", 0), T["iw"][:, :].indirect(T["b%d" % t][:, 0:18]), ["iw", "b%d.o" % t], ["jj0"])
+            copy("v", T["bu"][:, :], T["b0"][:, 0:18], ["b0.o"], ["bu"])
+            copy("s", part("jj", 0), T["iw"][:, :].indirect(T["bu"][:, :]), ["iw", "bu"], ["jj0"])
+
+        def m(k, q):
+            if k == 1: return tt(part("kk", 1), part("jj", 0), ci[:, :], A.min, ["jj0", "ci"], ["kk1"])
+            other = ("cc" if base[k] == k - 1 else "kk", base[k])
+            tt(part("kk", k), part("kk", k - 1).indirect(lo(stage[k])), part(*other), A.min, ["kk%d" % (k - 1), "lo%d" % stage[k], "%s%d" % other], ["kk%d" % k])
+
+        def c(k, q): copy(q, part("cc", k), part("kk", k), ["kk%d" % k], ["cc%d" % k])
+
+        def w(i, q):
+            src = "kk" if i == len(RAD) else "jj"
+            scan(part("zj", i % 2), part(src, wsrc[i]), ["%s%d" % (src, wsrc[i])], ["zj%d" % (i % 2)])
+
+        def o(i, q): rounded(lo(i), i % 2, ["lo%d" % i])
+
+        def d(k, q):
+            if k == 0: ts(T["bf"][:, :], T["b%d" % t][:, :], 0.25, None, A.add, None, ["b%d.o" % t, "b%d.i" % t], ["bf"])
+            else: tt(T["df"][:, :], T["bf"][:, :], T["af%d" % t][:, :], A.subtract, ["bf", "af%d.0" % t, "af%d.1" % t], ["df"])
+
+        def l(k, q):
+            for b in range(4): mm(bank("pr", b), part("wq", b, 128), part("wp", b, 128), T["rq%d" % p][:, :], T["rs%d" % p][:, :], ["wq", "wp", "rz%d" % p], ["pr%d" % b])
+
+        def a(b, q): tt(part("rr", b), bank("pr", b), part("gs", b), A.add, ["pr%d" % b, "gs%d" % b], ["rr%d" % b])
+
+        def x(b, q): copy(q, T["xt"][:, b:4 * C:4], part("rr", b).indirect(off(t, 1)), ["rr%d" % b, own + "1"], ["xt%d" % b], 2.0 ** -5)
+
+        def f(k, q):
+            if k == 0: call("s", lambda e: e.activation(T["fl"][:, :], bank("pr", 0), SIGN), ["pr0"], ["fl"])
+            else: call("s", lambda e: e.activation(T["flp"][:, :], T["fl"][:, :].indirect(off(t, 0)), RELU, scale=T["scol"][:, :]), ["fl", own + "0", "scol"], ["flp"])
+
+        def h(b, q): copy(q, part("fs", b), bank("pd", b), ["pd%d" % b], ["fs%d" % b])
+
+        def tf(k, q):
+            if k == 0: copy("s", part("tf", 0), T["flp"][:, :].indirect(lo(len(RAD))), ["flp", "lo%d" % len(RAD)], ["tf0"])
+            else: copy("s", part("tf", 1), part("tf", 0).indirect(off(t, 1)), ["tf0", own + "1"], ["tf1"])
+
+        def take(hh, k):
+            s, af = str(hh), "af%d.%d"
+            if k == 0: scan(part("zf", hh), part("tf", hh), ["tf" + s], ["zf" + s])
+            if k == 1: tt(part("fm", hh, 18), T["zf"][:, C * hh + 15:C * hh + C:16], part("df", hh, 18), A.mult, ["zf" + s, "df"], ["fm" + s])
+            if k == 2: tt(part("af%d" % n, hh, 18), part("fm", hh, 18), part("af%d" % t, hh, 18), A.add, ["fm" + s, af % (t, hh)], [af % (n, hh)])
+            if k == 3:
+                copy("v", off(n, hh), part("af%d" % n, hh, 18), [af % (n, hh)], [nxt + s])
+                name = "h%s%d" % ("wx"[hh], n)
+                if n < 3: send([nxt + s], (_helpers(core, dests[n], topo)[2 * hh], T[name][:, :], off(n, hh), name, es))
+
+        def g_(b, q): copy(q, part("gs", b), part("fs", b).indirect(off(n, 0)), ["fs%d" % b, nxt + "0"], ["gs%d" % b])
+
+        def y(b, q): tt(part("ys", b), part("gs", b), bank("pd", b), A.add, ["gs%d" % b, "pd%d" % b], ["ys%d" % b])
+
+        def z(b, q): copy(q, T["zt"][:, b:4 * C:4], part("ys", b).indirect(off(n, 0)), ["ys%d" % b, nxt + "0"], ["zt%d" % b], 2.0 ** -6)
+
+        def i_(k, q):
+            if n < 3: copy("s", T["iw"][:, :], ci[:, :].indirect(off(n, 1)), ["ci", nxt + "1"], ["iw"])
+
+        def r(k, q):
+            zq, zs, hq, half = T["zq%d" % t], T["zs%d" % t], T["hq%d" % t], C // 2
+            quant(zq[:, :], zs[:, :], T["zt"][:, :], ["zt0", "zt1", "zt2", "zt3"], ["z%d" % t])
+            ha, hb, hc = _helpers(core, dests[t], topo)
+            left = "sz" if n == 3 else "sent"
+            send(["z%d" % t], (ha, hq[:, 0:half].bitcast(dt.uint8), zq[:, 0:half].bitcast(dt.uint8), "hq%d" % t, es[1::2]),
+                 (hb, hq[:, half:C].bitcast(dt.uint8), zq[:, half:C].bitcast(dt.uint8), "hq%d" % t, es[0::2]), left=left)
+            send(["z%d" % t], (hc, T["hs%d" % t][:, :], zs[:, :], "hs%d" % t, es), left=left)
+
+        def e_(k, q):
+            quant(T["vq"][:, :], T["vp"][:, :], T["vin"][:, :], ["vin"], ["v"])
+            copy("s", T["fr"][:, :], iot[:, :].indirect(off(3, 0)), ["iot", "aw3.0"], ["fr"])
+            arrived(["z gone"], ("sz", sent["sz"]))
+            for k in range(8): store("y", T.fo[k:k + 1, :], T["fr"][16 * k:16 * k + 1, :], ["fr", "z gone"])
+        return {"j": j, "m": m, "c": c, "w": w, "o": o, "d": d, "l": l, "a": a, "x": x, "q": lambda k, q: state(t), "f": f, "h": h, "t": tf,
+                "k": lambda k, q: take(0, k), "p": lambda k, q: take(1, k), "g": g_, "y": y, "z": z, "i": i_, "r": r, "e": e_}
+
+    def run(t, order):
+        for s in order.split(): steps(t - (s[0] in "pgyzir"))[s[0]](int(s[1]), s[2:])
 
     for b in range(4): ts(T["et"][:, 512 * b + b:512 * b + 512:4], iot[:, 0:128], T["p1"][:, :], 32.0, A.is_equal, A.mult, ["iot", "p1", "et"], ["et%d" % b])
     ts(T["uof"][:, :], iot[:, 0:8], 16.0, None, A.mult, None, ["iot"], ["uof"])
-    copy("v", off(0, "o"), T["odi"][:, :], ["odi"], ["aw0.o"])
-    copy("v", T["iw0"][:, :].indirect(off(0, "o")), ci[:, :], ["ci", "aw0.o"], ["iw0"])
-    wrap("iw0", off(0, "i"), ["aw0.i"])
-    copy("v", T["ivi"][:, :], off(0, "i"), ["aw0.i"], ["ivi"])
-    send(["ivi"], (hb, T["hiv"][:, 0:9], T["ivi"][:, 0:9], "hiv", es[0::4]), (hc, T["hiv"][:, 9:18], T["ivi"][:, 9:18], "hiv", es[2::4]))
-    quant(T["eq"][:, :], T["ep"][:, :], T["et"][:, :], ["et0", "et1", "et2", "et3"], ["e"])
-    quant(T["xq0"][:, :], T["xs0"][:, :], T["xin"][:, :], ["xin"], ["x0"])
-    for b in range(4): unpack(0, b)
-    for b in range(4): held("s", b)
+    copy("v", off(0, 0), T["odi"][:, :], ["odi"], ["aw0.0"])
     quant(T["uq"][:, :], T["up"][:, :], T["uin"][:, :], ["uin"], ["u"])
+    quant(T["eq"][:, :], T["ep"][:, :], T["et"][:, :], ["et0", "et1", "et2", "et3"], ["e"])
     copy("v", T["urq"][:, :].bitcast(dt.uint32), T["uq"][:, :].bitcast(dt.uint32).indirect(T["uof"][:, :]), ["u", "uof"], ["urq"])
-    copy("v", T["urp"][:, :], T["up"][:, :].indirect(T["uof"][:, :]), ["u", "uof"], ["urp"])
-    score(0)
-    signs(0)
-    for h in (0, 1): own(0, h)
-
-    def small(t):
-        calls = others(t, 0) + others(t, 1)
-        return {(k, "scan"): [calls[k]] for k in range(6)}
-    chase(0, small(0))
-    choose(0)
-    means(0)
-    for t in (1, 2):
-        p = t - 1
-        plan = small(t)
-        plan[(5, "step")] = [lambda: layer(p)]
-        plan[(5, "min1")] = [lambda: summed(0)]
-        plan[(5, "twin")] = "v"
-        plan[(5, "off")] = [lambda: summed(1), lambda: moved(p, "s", 0), lambda: moved(p, "s", 1)]
-        plan[(6, "min0")] = [lambda: summed(2), lambda: summed(3), lambda: moved(p, "s", 2)]
-        plan[(6, "min1")] = [lambda: moved(p, "v", 3), lambda: state(t), lambda: signs(t)]
-        chase(t, plan)
-        for b in range(4): held("v", b)
-        choose(t)
-        means(t)
-    quant(T["vq"][:, :], T["vp"][:, :], T["vin"][:, :], ["vin"], ["v"])
-    copy("s", T["fr"][:, :], iot[:, :].indirect(off(3, "o")), ["iot", "aw3.o"], ["fr"])
-    for k in range(8): store("y", T.fo[k:k + 1, :], T["fr"][16 * k:16 * k + 1, :], ["fr"])
-    layer(2)
-    for b in range(4): summed(b)
-    for q, b in (("s", 0), ("s", 1), ("s", 2), ("v", 3)): moved(2, q, b)
-    state(3)
+    copy("s", T["urp"][:, :], T["up"][:, :].indirect(T["uof"][:, :]), ["u", "uof"], ["urp"])
+    run(0, "q0 f0 f1 h0s h1s h2s h3s")
+    copy("v", T["iw"][:, :].indirect(off(0, 0)), ci[:, :], ["ci", "aw0.0"], ["iw"])
+    scan(part("zj", 0), T["iw"][:, :], ["iw"], ["zj0"])
+    rounded(off(0, 1), 0, ["aw0.1"])
+    copy("v", T["ivi"][:, :], off(0, 1), ["aw0.1"], ["ivi"])
+    send(["ivi"], (hb, T["hiv"][:, 0:9], T["ivi"][:, 0:9], "hiv", rest[:8]), (hc, T["hiv"][:, 9:18], T["ivi"][:, 9:18], "hiv", rest[8:]), left="sod")
+    arrived(["lists gone"], ("sod", sent["sod"]))
+    load("y", T["wq"][:, :].bitcast(dt.uint8), T.wc[:, :], "lwc", ["wq"], ["lists gone"])
+    load("y", T["wp"][:, :], T.ws[:, :], "lws", ["wp"])
+    load("y", T["vin"][:, :], T.v[:, :], "lv", ["vin"])
+    ts(T["af0"][:, :], T["aw0"][:, :], 0.25, None, A.add, None, ["aw0.0", "aw0.1"], ["af0.0", "af0.1"])
+    for t, order in enumerate((FIRST, LATER, LATER, LAST)): run(t, order)
+    half = C // 2
+    for k in range(2): mm(bank("pr", k, half), T["vq"][:, :], T["vp"][:, :], part("xq3", k, half), part("xs3", k, half), ["v", "x3"], ["pr%d" % k])
+    for k, q in ((0, "v"), (1, "s")): copy(q, part("yo", k, half), bank("pr", k, half), ["pr%d" % k], ["yo%d" % k])
     store("y", T.oc[:, :], T["xq3"][:, :].bitcast(dt.uint8), ["x3"])
-    h = C // 2
-    for k in range(2): mm(bank("pr", k, h), T["vq"][:, :], T["vp"][:, :], T["xq3"][:, h * k:h * k + h], T["xs3"][:, h * k:h * k + h], ["v", "x3"], ["pr%d" % k])
-    for k in range(4): store("y" if k < 2 else "s", T.osc[4 * k:4 * k + 4, :], T["xs3"][32 * k:32 * k + 4, :], ["x3"])
-    copy("v", T["yo"][:, 0:h], bank("pr", 0, h), ["pr0"], ["yo0"])
-    copy("s", T["yo"][:, h:C], bank("pr", 1, h), ["pr1"], ["yo1"])
-    store("y", T.y[:, 0:h], T["yo"][:, 0:h], ["yo0"])
-    store("s", T.y[:, h:C], T["yo"][:, h:C], ["yo1"])
+    for k, q in ((0, "y"), (1, "s")):
+        if k: store(q, T.y[:, half:C], part("yo", 1, half), ["yo1"])
+        for m in (2 * k, 2 * k + 1): store(q, T.osc[4 * m:4 * m + 4, :], T["xs3"][32 * m:32 * m + 4, :], ["x3"])
+        if not k: store(q, T.y[:, 0:half], part("yo", 0, half), ["yo0"])
     for s in ("cv", "cs", "ct", "cg", "store"): g.wait_ge(T.sem[s], count[s])
     for s in sent: g.wait_ge(T.sem[s], sent[s])

@@ -6,14 +6,17 @@ STEP = [4, 1, 2]
 RAD = [2, 2, 2, 2, 2, 3, 3]
 F32, BF, I32, U16, U8, MX = "float32", "bfloat16", "int32", "uint16", "uint8", "float8_e4m3fn_x4"
 
-FIRST = ("j0 w0 o0 j1 m1 c1s w1 o1 j2 m2 c2s w2 o2 j3 m3 c3s w3 o3 j4 m4 c4s w4 o4 j5 m5 c5s w5 o5 "
-         "j6 m6 j7 m7 c7s w6 d0 o6 m8 m9 w7 d1 o7 t0 t1 k0 k1 k2 k3")
-LATER = ("p0 g0v g1s p1 y1 y0 g3s g2s p2 y3 z0s p3 i0 y2 z1v z3v z2s j0 r0 "
-         "w0 o0 j1 m1 c1s w1 o1 j2 m2 c2s w2 o2 l0 j3 m3 c3s w3 d0 o3 j4 m4 d1 c4s w4 o4 "
+FIRST = ("j0 f1 c0s w0 o0 j1 m1 c1s w1 o1 j2 m2 c2s w2 o2 j3 m3 c3s w3 o3 j4 m4 c4s w4 o4 j5 m5 c5s w5 o5 "
+         "j6 m6 j7 m7 c7s w6 d0 o6 m8 d1 m9 t1 k0 k4 k5 P0 k1 P4 k2 P5 k3 P1")
+MEANS0 = "g0v g1s p2 y1 p3 y0 g3s g2s y3 i0 z0s y2 z1v z3v z2s "
+MEANS1 = "p0 g0v g1s p1 y1 y0 g3s g2s p2 y3 z0s p3 i0 y2 z1v z3v z2s "
+LATER = ("j0 r0 w0 o0 j1 m1 c1s w1 o1 j2 m2 c2s w2 o2 l0 j3 m3 c3s w3 d0 o3 j4 m4 d1 c4s w4 o4 "
          "j5 m5 a0 c5s w5 a2 o5 a3 x0s j6 m6 a1 j7 m7 x3s x1s w6 x2v o6 q0 c7s m8 f0 m9 w7 o7 "
          "h1v f1 h2s t0 h0v k0 k1 h3s k2 k3 t1")
-LAST = ("g0v g1s g3s g2s y1 y0 y3 z0s y2 z1v z3s z2v r0 p0 p1 p2 p3 e0 "
-        "l0 a0 a1 a2 a3 x0s x1s x2s x3v q0")
+LAST = ("p0 g0s p1 g1s p2 g2s p3 g3v u0 H0v T0s H1v T1s H2v T2s H3v T3s "
+        "y0 y1 y2 y3 z0s z1s z2s z3v0 z3s1 r0 e0 "
+        "l0 a0 a1 a2 a3 x0s0 x1s0 x2s0 x3v0 q0 x0s1 x1s1 x3v1 x2s1 q1 v0s v1v s0y s1y s2y s3y")
+RUNS = ((0, 160), (160, C))
 
 
 def _scratch():
@@ -21,16 +24,17 @@ def _scratch():
 
     def sb(dtype, **names):
         for k in names: s[k] = ("sbuf", [128, names[k]], dtype)
-    sb(I32, odi=18, b0=36, ivi=18, hiv=18, pidx=1, p15=1)
+    sb(I32, odi=18, b0=36, ivi=18, hiv=18, zi=36, zb=36, pidx=1, p15=1)
     for k in ("odd", "hod"): s[k] = ("dram", [128, 18], I32)
-    sb(U16, ofc=18, uof=8, bu=18, lo=18 * 8, b1=36, b2=36)
+    sb(U16, ofc=18, uof=8, bu=18, lo=18 * 8, b1=36, b2=36, b3=18, hw3=18)
     for k in range(4): sb(U16, **{"aw%d" % k: 36})
     for k in (1, 2): sb(U16, **{a + "%d" % k: 18 for a in ("hw", "hx")})
     sb(BF, xin=4 * C, uin=512, vin=512, et=2048, zt=4 * C, xt=4 * C)
     sb(BF, ci=C, scc=C, jj=8 * C, kk=10 * C, cc=8 * C, zj=2 * C, fl=C, flp=C, tf=2 * C, zf=2 * C, iw=C)
+    sb(F32, kf=11 * C, cf=8 * C, i4=C, zk=2 * C)
     sb(F32, iot=C, p1=1, p16=1, sct=1, scol=1, ne=16, nx=16, t1=16, sc16=16)
     sb(F32, gs=4 * C, bf=36, df=36, fm=36, af0=36, af1=36, af2=36, af3=36)
-    sb(F32, fs=4 * C, ys=4 * C, rr=4 * C, yo=C, fr=C)
+    sb(F32, fs=4 * C, ys=4 * C, rr=4 * C, fp=4 * C, fq=4 * C, yo=C, fr=C)
     for k, n in (("w", 512), ("e", 512), ("u", 128), ("ur", 128), ("v", 128)): sb(MX, **{k + "q": n}); sb(U8, **{k + "p": n})
     for k in range(4): sb(MX, **{"xq%d" % k: C}); sb(U8, **{"xs%d" % k: C})
     for k in range(3):
@@ -42,7 +46,7 @@ def _scratch():
 
 SCRATCH = _scratch()
 SEMAPHORES = ["cv", "cs", "ct", "cg", "lod", "lodd", "lx", "lu", "lv", "lwc", "lws", "store", "sent", "sod", "sz",
-              "hod", "hiv", "hw1", "hw2", "hx1", "hx2", "rx1", "rx2", "hq0", "hq1", "hq2", "hs0", "hs1", "hs2",
+              "hod", "hiv", "hw1", "hw2", "hw3", "rw3", "hx1", "hx2", "rx1", "rx2", "hq0", "hq1", "hq2", "hs0", "hs1", "hs2",
               "roda", "rivb", "rivc", "rw1", "rw2", "rqa0", "rqa1", "rqa2", "rqb0", "rqb1", "rqb2", "rs0", "rs1", "rs2"]
 
 
@@ -92,6 +96,9 @@ def _relay(g, core, rc, T, topo):
             k = "s%d" % t
             g.wait_ge(T.sem["h" + k], on_chip(1))
             n += fwd(dest, T["r" + k][:, :], T["h" + k][:, :], "r" + k)
+            if t == 2:
+                g.wait_ge(T.sem["hw3"], on_chip(1))
+                n += fwd(dest, T["b3"][:, :], T["hw3"][:, :], "rw3")
     if n: g.wait_ge(T.sem["sent"], n)
 
 
@@ -187,8 +194,10 @@ def rank_program(g, core, T, topo):
     call("g", lambda e: e.iota(T["pidx"][:, :], [[1, 1]], 0, 1), [], ["pidx"])
     call("g", lambda e: e.iota(iot[:, :], [[1, C]], 0, 0, allow_small_or_imprecise_dtypes=True), [], ["iot"])
     send(["odd"], (ha, T["hod"][:, :], T["odd"][:, :], "hod", es[1::4]), left="sod")
+    call("g", lambda e: e.iota(T["i4"][:, :], [[4, C]], 1, 0, allow_small_or_imprecise_dtypes=True), [], ["i4"])
     arrived(["b0.o"], ("roda", back[0][0]))
     arrived(["b0.i"], ("rivb", back[0][1]), ("rivc", back[0][2]))
+    arrived(["b3.o"], ("rw3", back[2][2]))
     for t in range(3):
         if t:
             arrived(["b%d.o" % t], ("rw%d" % t, back[t][0]))
@@ -216,13 +225,14 @@ def rank_program(g, core, T, topo):
 
     def rounded(out, z, writes): ts(out, T["zj"][:, C * z + 15:C * z + C:16], T["scol"][:, :], 144.25, A.mult, A.add, ["zj%d" % z, "scol"], writes)
 
+    def whole(tile): return ["%s%d.%d" % (tile, b, k) for b in range(4) for k in (0, 1)]
+
     def state(n):
         q, s = T["xq%d" % n], T["xs%d" % n]
-        if n: quant(q[:, :], s[:, :], T["xt"][:, :], ["xt0", "xt1", "xt2", "xt3"], ["x%d" % n])
+        if n: quant(q[:, :], s[:, :], T["xt"][:, :], whole("xt"), ["x%d" % n])
         else: quant(q[:, :], s[:, :], T["xin"][:, :], ["xin"], ["x0"])
-        if n < 3:
-            mm(bank("pr", 0), T["urq"][:, :], T["urp"][:, :], q[:, :], s[:, :], ["urq", "urp", "x%d" % n], ["pr0"])
-            for b in range(4): mm(bank("pd", b), part("eq", b, 128), part("ep", b, 128), q[:, :], s[:, :], ["e", "x%d" % n], ["pd%d" % b])
+        mm(bank("pr", 0), T["urq"][:, :], T["urp"][:, :], q[:, :], s[:, :], ["urq", "urp", "x%d" % n], ["pr0"])
+        for b in range(4): mm(bank("pd", b), part("eq", b, 128), part("ep", b, 128), q[:, :], s[:, :], ["e", "x%d" % n], ["pd%d" % b])
 
     stage, base, wsrc = [None], [None], [0]
     for i, r in enumerate(RAD):
@@ -234,6 +244,8 @@ def rank_program(g, core, T, topo):
         n, p = t + 1, t - 1
         own, nxt = "aw%d." % t, "aw%d." % n
 
+        kk, cc = ("kk", "cc") if t else ("kf", "cf")
+
         def lo(i): return part("lo", i, 18)
 
         def j(k, q):
@@ -243,11 +255,11 @@ def rank_program(g, core, T, topo):
             copy("s", part("jj", 0), T["iw"][:, :].indirect(T["bu"][:, :]), ["iw", "bu"], ["jj0"])
 
         def m(k, q):
-            if k == 1: return tt(part("kk", 1), part("jj", 0), ci[:, :], A.min, ["jj0", "ci"], ["kk1"])
-            other = ("cc" if base[k] == k - 1 else "kk", base[k])
-            tt(part("kk", k), part("kk", k - 1).indirect(lo(stage[k])), part(*other), A.min, ["kk%d" % (k - 1), "lo%d" % stage[k], "%s%d" % other], ["kk%d" % k])
+            if k == 1 and t: return tt(part(kk, 1), part("jj", 0), ci[:, :], A.min, ["jj0", "ci"], ["kk1"])
+            other = (cc if base[k] == k - 1 else kk, base[k])
+            tt(part(kk, k), part(kk, k - 1).indirect(lo(stage[k])), part(*other), A.min, [kk + str(k - 1), "lo%d" % stage[k], "%s%d" % other], [kk + str(k)])
 
-        def c(k, q): copy(q, part("cc", k), part("kk", k), ["kk%d" % k], ["cc%d" % k])
+        def c(k, q): copy(q, part(cc, k), part(kk, k), [kk + str(k)], [cc + str(k)])
 
         def w(i, q):
             src = "kk" if i == len(RAD) else "jj"
@@ -259,58 +271,103 @@ def rank_program(g, core, T, topo):
             if k == 0: ts(T["bf"][:, :], T["b%d" % t][:, :], 0.25, None, A.add, None, ["b%d.o" % t, "b%d.i" % t], ["bf"])
             else: tt(T["df"][:, :], T["bf"][:, :], T["af%d" % t][:, :], A.subtract, ["bf", "af%d.0" % t, "af%d.1" % t], ["df"])
 
+        zq, zs, zr, lb = ("zq2", "zs2", "z2", "pd") if t == 3 else ("rq%d" % p, "rs%d" % p, "rz%d" % p, "pr")
+
         def l(k, q):
-            for b in range(4): mm(bank("pr", b), part("wq", b, 128), part("wp", b, 128), T["rq%d" % p][:, :], T["rs%d" % p][:, :], ["wq", "wp", "rz%d" % p], ["pr%d" % b])
+            for b in range(4): mm(bank(lb, b), part("wq", b, 128), part("wp", b, 128), T[zq][:, :], T[zs][:, :], ["wq", "wp", zr], [lb + str(b)])
 
-        def a(b, q): tt(part("rr", b), bank("pr", b), part("gs", b), A.add, ["pr%d" % b, "gs%d" % b], ["rr%d" % b])
+        def a(b, q): tt(part("rr", b), bank(lb, b), part("gs", b), A.add, [lb + str(b), "gs%d" % b], ["rr%d" % b])
 
-        def x(b, q): copy(q, T["xt"][:, b:4 * C:4], part("rr", b).indirect(off(t, 1)), ["rr%d" % b, own + "1"], ["xt%d" % b], 2.0 ** -5)
+        def moved(q, tile, b, src, offsets, first, region, scale):
+            runs = [int(q[1])] if len(q) > 1 else [0, 1]
+            c0, c1 = RUNS[runs[0]][0], RUNS[runs[-1]][1]
+            copy(q[0], T[tile][:, 4 * c0 + b:4 * c1:4], part(src, b).indirect(T[offsets][:, first + c0 // 16:first + c1 // 16]), [src + str(b), region],
+                 ["%s%d.%d" % (tile, b, k) for k in runs], scale)
+
+        def x(b, q): moved(q, "xt", b, "rr", "aw%d" % t, 18, own + "1", 2.0 ** -5)
 
         def f(k, q):
             if k == 0: call("s", lambda e: e.activation(T["fl"][:, :], bank("pr", 0), SIGN), ["pr0"], ["fl"])
+            elif t == 0: tt(part("kf", 0), T["fl"][:, :].indirect(off(0, 0)), T["i4"][:, :], A.add, ["fl", "aw0.0", "i4"], ["kf0"])
             else: call("s", lambda e: e.activation(T["flp"][:, :], T["fl"][:, :].indirect(off(t, 0)), RELU, scale=T["scol"][:, :]), ["fl", own + "0", "scol"], ["flp"])
 
         def h(b, q): copy(q, part("fs", b), bank("pd", b), ["pd%d" % b], ["fs%d" % b])
 
         def tf(k, q):
-            if k == 0: copy("s", part("tf", 0), T["flp"][:, :].indirect(lo(len(RAD))), ["flp", "lo%d" % len(RAD)], ["tf0"])
+            if t == 0: copy("s", part("kf", 10), part("kf", 9).indirect(off(0, 1)), ["kf9", "aw0.1"], ["kf10"])
+            elif k == 0: copy("s", part("tf", 0), T["flp"][:, :].indirect(lo(len(RAD))), ["flp", "lo%d" % len(RAD)], ["tf0"])
             else: copy("s", part("tf", 1), part("tf", 0).indirect(off(t, 1)), ["tf0", own + "1"], ["tf1"])
 
         def take(hh, k):
             s, af = str(hh), "af%d.%d"
-            if k == 0: scan(part("zf", hh), part("tf", hh), ["tf" + s], ["zf" + s])
-            if k == 1: tt(part("fm", hh, 18), T["zf"][:, C * hh + 15:C * hh + C:16], part("df", hh, 18), A.mult, ["zf" + s, "df"], ["fm" + s])
+            src, wrapped = (("tf", hh), "zf") if t else (("kf", 9 + hh), "zk")
+            ends = T[wrapped][:, C * hh + 15:C * hh + C:16]
+            if k == 0: scan(part(wrapped, hh), part(*src), ["%s%d" % src], ["zf" + s])
+            if k == 4: ts(part("zi", hh, 18), ends, T["scol"][:, :], 0.25, A.mult, A.add, ["zf" + s, "scol"], ["zi" + s])
+            if k == 5: ts(part("zb", hh, 18), part("zi", hh, 18), 1, 1, A.logical_shift_right, A.bitwise_and, ["zi" + s], ["zb" + s])
+            if k == 1: tt(part("fm", hh, 18), ends if t else part("zb", hh, 18), part("df", hh, 18), A.mult, [("zf" if t else "zb") + s, "df"], ["fm" + s])
             if k == 2: tt(part("af%d" % n, hh, 18), part("fm", hh, 18), part("af%d" % t, hh, 18), A.add, ["fm" + s, af % (t, hh)], [af % (n, hh)])
             if k == 3:
                 copy("v", off(n, hh), part("af%d" % n, hh, 18), [af % (n, hh)], [nxt + s])
                 name = "h%s%d" % ("wx"[hh], n)
                 if n < 3: send([nxt + s], (_helpers(core, dests[n], topo)[2 * hh], T[name][:, :], off(n, hh), name, es))
+                elif hh == 0: send([nxt + s], (_helpers(core, dests[t], topo)[2], T[name][:, :], off(n, hh), name, es), left="sz")
 
         def g_(b, q): copy(q, part("gs", b), part("fs", b).indirect(off(n, 0)), ["fs%d" % b, nxt + "0"], ["gs%d" % b])
 
-        def y(b, q): tt(part("ys", b), part("gs", b), bank("pd", b), A.add, ["gs%d" % b, "pd%d" % b], ["ys%d" % b])
+        zo, ro = ("b3", "b3.o") if n >= 3 else ("aw%d" % n, nxt + "0")
 
-        def z(b, q): copy(q, T["zt"][:, b:4 * C:4], part("ys", b).indirect(off(n, 0)), ["ys%d" % b, nxt + "0"], ["zt%d" % b], 2.0 ** -6)
+        def u(k, q):
+            for b in range(4): mm(bank("pr", b), part("eq", b, 128), part("ep", b, 128), T["rq2"][:, :], T["rs2"][:, :], ["e", "rz2"], ["pr%d" % b])
 
-        def i_(k, q):
-            if n < 3: copy("s", T["iw"][:, :], ci[:, :].indirect(off(n, 1)), ["ci", nxt + "1"], ["iw"])
+        def hp(b, q): copy(q, part("fp", b), bank("pr", b), ["pr%d" % b], ["fp%d" % b])
+
+        def tp(b, q): copy(q, part("fq", b), part("fp", b), ["fp%d" % b], ["fq%d" % b])
+
+        def y(b, q):
+            if n < 3: tt(part("ys", b), part("gs", b), bank("pd", b), A.add, ["gs%d" % b, "pd%d" % b], ["ys%d" % b])
+            else: tt(part("ys", b), part("fp", b).indirect(T[zo][:, :]), part("fq", b), A.add, ["fp%d" % b, "fq%d" % b, ro], ["ys%d" % b])
+
+        def z(b, q): moved(q, "zt", b, "ys", zo, 0, ro, 2.0 ** -6)
+
+        def i_(k, q): copy("s", T["iw"][:, :], ci[:, :].indirect(off(n, 1)), ["ci", nxt + "1"], ["iw"])
+
+        def codes(q, s, region):
+            hq, half = T["hq%d" % t], C // 2
+            ha, hb, hc = _helpers(core, dests[t], topo)
+            send([region], (ha, hq[:, 0:half].bitcast(dt.uint8), q[:, 0:half].bitcast(dt.uint8), "hq%d" % t, es[1::2]),
+                 (hb, hq[:, half:C].bitcast(dt.uint8), q[:, half:C].bitcast(dt.uint8), "hq%d" % t, es[0::2]))
+            send([region], (hc, T["hs%d" % t][:, :], s[:, :], "hs%d" % t, es))
 
         def r(k, q):
-            zq, zs, hq, half = T["zq%d" % t], T["zs%d" % t], T["hq%d" % t], C // 2
-            quant(zq[:, :], zs[:, :], T["zt"][:, :], ["zt0", "zt1", "zt2", "zt3"], ["z%d" % t])
-            ha, hb, hc = _helpers(core, dests[t], topo)
-            left = "sz" if n == 3 else "sent"
-            send(["z%d" % t], (ha, hq[:, 0:half].bitcast(dt.uint8), zq[:, 0:half].bitcast(dt.uint8), "hq%d" % t, es[1::2]),
-                 (hb, hq[:, half:C].bitcast(dt.uint8), zq[:, half:C].bitcast(dt.uint8), "hq%d" % t, es[0::2]), left=left)
-            send(["z%d" % t], (hc, T["hs%d" % t][:, :], zs[:, :], "hs%d" % t, es), left=left)
+            quant(T["zq%d" % t][:, :], T["zs%d" % t][:, :], T["zt"][:, :], whole("zt"), ["z%d" % t])
+            if n < 3: codes(T["zq%d" % t], T["zs%d" % t], "z%d" % t)
+
+        def q_(k, q):
+            if t < 3: state(t)
+            if t == 2: codes(T["xq2"], T["xs2"], "x2")
+            if t == 3:
+                c0, c1 = RUNS[k]
+                r = "x3.%d" % k
+                quant(T["xq3"][:, c0:c1], T["xs3"][:, c0:c1], T["xt"][:, 4 * c0:4 * c1], ["xt%d.%d" % (b, k) for b in range(4)], [r])
+                mm(bank("pr", k, c1 - c0), T["vq"][:, :], T["vp"][:, :], T["xq3"][:, c0:c1], T["xs3"][:, c0:c1], ["v", r], ["pr%d" % k])
+                store("y", T.oc[:, 4 * c0:4 * c1], T["xq3"][:, c0:c1].bitcast(dt.uint8), [r])
+
+        def v_(k, q):
+            c0, c1 = RUNS[k]
+            copy(q, T["yo"][:, c0:c1], bank("pr", k, c1 - c0), ["pr%d" % k], ["yo%d" % k])
+            if k: store("s", T.y[:, :], T["yo"][:, :], ["yo0", "yo1"])
+
+        def s_(m, q): store(q, T.osc[4 * m:4 * m + 4, :], T["xs3"][32 * m:32 * m + 4, :], ["x3.0", "x3.1"])
 
         def e_(k, q):
             quant(T["vq"][:, :], T["vp"][:, :], T["vin"][:, :], ["vin"], ["v"])
             copy("s", T["fr"][:, :], iot[:, :].indirect(off(3, 0)), ["iot", "aw3.0"], ["fr"])
-            arrived(["z gone"], ("sz", sent["sz"]))
-            for k in range(8): store("y", T.fo[k:k + 1, :], T["fr"][16 * k:16 * k + 1, :], ["fr", "z gone"])
-        return {"j": j, "m": m, "c": c, "w": w, "o": o, "d": d, "l": l, "a": a, "x": x, "q": lambda k, q: state(t), "f": f, "h": h, "t": tf,
-                "k": lambda k, q: take(0, k), "p": lambda k, q: take(1, k), "g": g_, "y": y, "z": z, "i": i_, "r": r, "e": e_}
+            arrived(["list gone"], ("sz", sent["sz"]))
+            for k in range(8): store("y", T.fo[k:k + 1, :], T["fr"][16 * k:16 * k + 1, :], ["fr", "list gone"])
+        return {"j": j, "m": m, "c": c, "w": w, "o": o, "d": d, "l": l, "a": a, "x": x, "q": q_, "f": f, "h": h, "t": tf,
+                "k": lambda k, q: take(0, k), "p": lambda k, q: take(1, k), "g": g_, "y": y, "z": z, "i": i_, "r": r, "e": e_,
+                "P": lambda k, q: take(1, k), "u": u, "H": hp, "T": tp, "v": v_, "s": s_}
 
     def run(t, order):
         for s in order.split(): steps(t - (s[0] in "pgyzir"))[s[0]](int(s[1]), s[2:])
@@ -322,7 +379,7 @@ def rank_program(g, core, T, topo):
     quant(T["eq"][:, :], T["ep"][:, :], T["et"][:, :], ["et0", "et1", "et2", "et3"], ["e"])
     copy("v", T["urq"][:, :].bitcast(dt.uint32), T["uq"][:, :].bitcast(dt.uint32).indirect(T["uof"][:, :]), ["u", "uof"], ["urq"])
     copy("s", T["urp"][:, :], T["up"][:, :].indirect(T["uof"][:, :]), ["u", "uof"], ["urp"])
-    run(0, "q0 f0 f1 h0s h1s h2s h3s")
+    run(0, "q0 f0 h0s h1s h2s h3s")
     copy("v", T["iw"][:, :].indirect(off(0, 0)), ci[:, :], ["ci", "aw0.0"], ["iw"])
     scan(part("zj", 0), T["iw"][:, :], ["iw"], ["zj0"])
     rounded(off(0, 1), 0, ["aw0.1"])
@@ -333,14 +390,6 @@ def rank_program(g, core, T, topo):
     load("y", T["wp"][:, :], T.ws[:, :], "lws", ["wp"])
     load("y", T["vin"][:, :], T.v[:, :], "lv", ["vin"])
     ts(T["af0"][:, :], T["aw0"][:, :], 0.25, None, A.add, None, ["aw0.0", "aw0.1"], ["af0.0", "af0.1"])
-    for t, order in enumerate((FIRST, LATER, LATER, LAST)): run(t, order)
-    half = C // 2
-    for k in range(2): mm(bank("pr", k, half), T["vq"][:, :], T["vp"][:, :], part("xq3", k, half), part("xs3", k, half), ["v", "x3"], ["pr%d" % k])
-    for k, q in ((0, "v"), (1, "s")): copy(q, part("yo", k, half), bank("pr", k, half), ["pr%d" % k], ["yo%d" % k])
-    store("y", T.oc[:, :], T["xq3"][:, :].bitcast(dt.uint8), ["x3"])
-    for k, q in ((0, "y"), (1, "s")):
-        if k: store(q, T.y[:, half:C], part("yo", 1, half), ["yo1"])
-        for m in (2 * k, 2 * k + 1): store(q, T.osc[4 * m:4 * m + 4, :], T["xs3"][32 * m:32 * m + 4, :], ["x3"])
-        if not k: store(q, T.y[:, 0:half], part("yo", 0, half), ["yo0"])
+    for t, order in enumerate((FIRST, MEANS0 + LATER, MEANS1 + LATER, LAST)): run(t, order)
     for s in ("cv", "cs", "ct", "cg", "store"): g.wait_ge(T.sem[s], count[s])
     for s in sent: g.wait_ge(T.sem[s], sent[s])

@@ -6,13 +6,13 @@ STEP = [4, 1, 2]
 RAD = [2, 2, 2, 2, 2, 3, 3]
 F32, BF, I32, U16, U8, MX = "float32", "bfloat16", "int32", "uint16", "uint8", "float8_e4m3fn_x4"
 
-FIRST = ("j0 f1 c0s w0 o0 j1 m1 c1s w1 o1 j2 m2 c2s w2 o2 j3 m3 c3s w3 o3 j4 m4 c4s w4 o4 j5 m5 c5s w5 o5 "
-         "j6 m6 j7 m7 c7s w6 d0 o6 m8 d1 m9 t1 k0 k4 k5 P0 k1 P4 k2 P5 k3 P1")
+FIRST = ("j0* f1 c0s w0* o0* j1* m1* c1s* w1* o1* j2* m2* c2s* w2* o2* j3* m3* c3s* w3* o3* j4* m4* c4s* w4* o4* j5* m5* c5s* w5* o5* "
+         "j6* m6* j7* m7* c7s* w6* o6* m8* d0 m9* d1 t1 k0* k4 k5 P0 k1 P4 k2 P5 k3 P1")
 MEANS0 = "g0v g1s p2 y1 p3 y0 g3s g2s y3 i0 z0s y2 z1v z3v z2s "
-MEANS1 = "p0 g0v g1s p1 y1 y0 g3s g2s p2 y3 z0s p3 i0 y2 z1v z3v z2s "
-LATER = ("j0 r0 w0 o0 j1 m1 c1s w1 o1 j2 m2 c2s w2 o2 l0 j3 m3 c3s w3 d0 o3 j4 m4 d1 c4s w4 o4 "
-         "j5 m5 a0 c5s w5 a2 o5 a3 x0s j6 m6 a1 j7 m7 x3s x1s w6 x2v o6 q0 c7s m8 f0 m9 w7 o7 "
-         "h1v f1 h2s t0 h0v k0 k1 h3s k2 k3 t1")
+MEANS1 = "p0 g0v g1s p1 y1 p2 y0 g3s g2s p3 y3 z0s i0 y2 z1v z3v z2s "
+LATER = ("j0* r0 w0* o0* j1* m1* c1s* w1* o1* j2* m2* c2s* w2* o2* l0 j3* m3* c3s* w3* o3* d0 j4* m4* c4s* w4* o4* j5* m5* "
+         "a0 c5s w5 a1 o5 a2 a3 x0s j6 m6 x3v x1s j70 x2s j71 m7 c7s* w60 q0 w61 o6* m8* f0 h0s f1 d1 m9* w7* o7* "
+         "h1s h2s h3s t0v* k0* k1 k2 k3 t1")
 LAST = ("p0 g0s p1 g1s p2 g2s p3 g3v u0 H0v T0s H1v T1s H2v T2s H3v T3s "
         "y0 y1 y2 y3 z0s z1s z2s z3v0 z3s1 r0 e0 "
         "l0 a0 a1 a2 a3 x0s0 x1s0 x2s0 x3v0 q0 x0s1 x1s1 x3v1 x2s1 q1 v0s v1v s0y s1y s2y s3y")
@@ -158,8 +158,6 @@ def rank_program(g, core, T, topo):
         elif scale == 1.0: call("v", lambda e: e.tensor_copy(out, in_), reads, writes)
         else: ts(out, in_, scale, None, A.mult, None, reads, writes)
 
-    def scan(out, in_, reads, writes): call("v", lambda e: e.tensor_tensor_scan(out, T["scc"][:, :], in_, 0.0, A.mult, A.add), ["scc"] + reads, writes)
-
     def quant(q, s, in_, reads, writes): call("v", lambda e: e.quantize_mx(q, s, in_), reads, writes)
 
     def mm(out, lq, ls, rq, rs, reads, writes): call("t", lambda e: e.matmul_mx(out, lq, ls, rq, rs, True, True), reads, writes)
@@ -223,9 +221,23 @@ def rank_program(g, core, T, topo):
 
     def off(t, h): return part("aw%d" % t, h, 18)
 
-    def rounded(out, z, writes): ts(out, T["zj"][:, C * z + 15:C * z + C:16], T["scol"][:, :], 144.25, A.mult, A.add, ["zj%d" % z, "scol"], writes)
+    def runs(q):
+        ks = [int(q[-1])] if q[-1:].isdigit() else [0, 1]
+        return ks, RUNS[ks[0]][0], RUNS[ks[-1]][1]
 
-    def whole(tile): return ["%s%d.%d" % (tile, b, k) for b in range(4) for k in (0, 1)]
+    def cols(name, k, q): return T[name][:, C * k + runs(q)[1]:C * k + runs(q)[2]]
+
+    def offs(name, first, q): return T[name][:, first + runs(q)[1] // 16:first + runs(q)[2] // 16]
+
+    def reg(name, k, q=""): return ["%s%d.%d" % (name, k, r) for r in runs(q)[0]]
+
+    def scan(out, ko, src, k, q=""):
+        call("v", lambda e: e.tensor_tensor_scan(cols(out, ko, q), cols("scc", 0, q), cols(src, k, q), 0.0, A.mult, A.add), ["scc"] + reg(src, k, q), reg(out, ko, q))
+
+    def rounded(out, z, writes, q=""):
+        ts(out, T["zj"][:, C * z + runs(q)[1] + 15:C * z + runs(q)[2]:16], T["scol"][:, :], 144.25, A.mult, A.add, reg("zj", z, q) + ["scol"], writes)
+
+    def whole(tile): return [r for b in range(4) for r in reg(tile, b)]
 
     def state(n):
         q, s = T["xq%d" % n], T["xs%d" % n]
@@ -246,26 +258,25 @@ def rank_program(g, core, T, topo):
 
         kk, cc = ("kk", "cc") if t else ("kf", "cf")
 
-        def lo(i): return part("lo", i, 18)
-
         def j(k, q):
-            if k: return copy("s", part("jj", k), part("jj", k - 1).indirect(lo(stage[k])), ["jj%d" % (k - 1), "lo%d" % stage[k]], ["jj%d" % k])
-            if t: return copy("s", part("jj", 0), T["iw"][:, :].indirect(T["b%d" % t][:, 0:18]), ["iw", "b%d.o" % t], ["jj0"])
-            copy("v", T["bu"][:, :], T["b0"][:, 0:18], ["b0.o"], ["bu"])
-            copy("s", part("jj", 0), T["iw"][:, :].indirect(T["bu"][:, :]), ["iw", "bu"], ["jj0"])
+            if k: return copy("s", cols("jj", k, q), part("jj", k - 1).indirect(offs("lo", 18 * stage[k], q)), reg("jj", k - 1) + reg("lo", stage[k], q), reg("jj", k, q))
+            if t: return copy("s", cols("jj", 0, q), T["iw"][:, :].indirect(offs("b%d" % t, 0, q)), ["iw", "b%d.o" % t], reg("jj", 0, q))
+            if 0 in runs(q)[0]: copy("v", T["bu"][:, :], T["b0"][:, 0:18], ["b0.o"], ["bu"])
+            copy("s", cols("jj", 0, q), T["iw"][:, :].indirect(offs("bu", 0, q)), ["iw", "bu"], reg("jj", 0, q))
 
         def m(k, q):
-            if k == 1 and t: return tt(part(kk, 1), part("jj", 0), ci[:, :], A.min, ["jj0", "ci"], ["kk1"])
+            if k == 1 and t: return tt(cols(kk, 1, q), cols("jj", 0, q), cols("ci", 0, q), A.min, reg("jj", 0, q) + ["ci"], reg(kk, 1, q))
             other = (cc if base[k] == k - 1 else kk, base[k])
-            tt(part(kk, k), part(kk, k - 1).indirect(lo(stage[k])), part(*other), A.min, [kk + str(k - 1), "lo%d" % stage[k], "%s%d" % other], [kk + str(k)])
+            tt(cols(kk, k, q), part(kk, k - 1).indirect(offs("lo", 18 * stage[k], q)), cols(*other, q), A.min,
+               reg(kk, k - 1) + reg("lo", stage[k], q) + reg(*other, q), reg(kk, k, q))
 
-        def c(k, q): copy(q, part(cc, k), part(kk, k), [kk + str(k)], [cc + str(k)])
+        def c(k, q): copy(q[0], cols(cc, k, q), cols(kk, k, q), reg(kk, k, q), reg(cc, k, q))
 
         def w(i, q):
             src = "kk" if i == len(RAD) else "jj"
-            scan(part("zj", i % 2), part(src, wsrc[i]), ["%s%d" % (src, wsrc[i])], ["zj%d" % (i % 2)])
+            scan("zj", i % 2, src, wsrc[i], q)
 
-        def o(i, q): rounded(lo(i), i % 2, ["lo%d" % i])
+        def o(i, q): rounded(offs("lo", 18 * i, q), i % 2, reg("lo", i, q), q)
 
         def d(k, q):
             if k == 0: ts(T["bf"][:, :], T["b%d" % t][:, :], 0.25, None, A.add, None, ["b%d.o" % t, "b%d.i" % t], ["bf"])
@@ -279,33 +290,31 @@ def rank_program(g, core, T, topo):
         def a(b, q): tt(part("rr", b), bank(lb, b), part("gs", b), A.add, [lb + str(b), "gs%d" % b], ["rr%d" % b])
 
         def moved(q, tile, b, src, offsets, first, region, scale):
-            runs = [int(q[1])] if len(q) > 1 else [0, 1]
-            c0, c1 = RUNS[runs[0]][0], RUNS[runs[-1]][1]
-            copy(q[0], T[tile][:, 4 * c0 + b:4 * c1:4], part(src, b).indirect(T[offsets][:, first + c0 // 16:first + c1 // 16]), [src + str(b), region],
-                 ["%s%d.%d" % (tile, b, k) for k in runs], scale)
+            ks, c0, c1 = runs(q)
+            copy(q[0], T[tile][:, 4 * c0 + b:4 * c1:4], part(src, b).indirect(offs(offsets, first, q)), [src + str(b), region], reg(tile, b, q), scale)
 
         def x(b, q): moved(q, "xt", b, "rr", "aw%d" % t, 18, own + "1", 2.0 ** -5)
 
         def f(k, q):
             if k == 0: call("s", lambda e: e.activation(T["fl"][:, :], bank("pr", 0), SIGN), ["pr0"], ["fl"])
-            elif t == 0: tt(part("kf", 0), T["fl"][:, :].indirect(off(0, 0)), T["i4"][:, :], A.add, ["fl", "aw0.0", "i4"], ["kf0"])
+            elif t == 0: tt(part("kf", 0), T["fl"][:, :].indirect(off(0, 0)), T["i4"][:, :], A.add, ["fl", "aw0.0", "i4"], reg("kf", 0))
             else: call("s", lambda e: e.activation(T["flp"][:, :], T["fl"][:, :].indirect(off(t, 0)), RELU, scale=T["scol"][:, :]), ["fl", own + "0", "scol"], ["flp"])
 
         def h(b, q): copy(q, part("fs", b), bank("pd", b), ["pd%d" % b], ["fs%d" % b])
 
         def tf(k, q):
-            if t == 0: copy("s", part("kf", 10), part("kf", 9).indirect(off(0, 1)), ["kf9", "aw0.1"], ["kf10"])
-            elif k == 0: copy("s", part("tf", 0), T["flp"][:, :].indirect(lo(len(RAD))), ["flp", "lo%d" % len(RAD)], ["tf0"])
-            else: copy("s", part("tf", 1), part("tf", 0).indirect(off(t, 1)), ["tf0", own + "1"], ["tf1"])
+            if t == 0: copy("s", part("kf", 10), part("kf", 9).indirect(off(0, 1)), reg("kf", 9) + ["aw0.1"], reg("kf", 10))
+            elif k == 0: copy(q[0], cols("tf", 0, q), T["flp"][:, :].indirect(offs("lo", 18 * len(RAD), q)), ["flp"] + reg("lo", len(RAD), q), reg("tf", 0, q))
+            else: copy("s", part("tf", 1), part("tf", 0).indirect(off(t, 1)), reg("tf", 0) + [own + "1"], reg("tf", 1))
 
-        def take(hh, k):
+        def take(hh, k, q):
             s, af = str(hh), "af%d.%d"
             src, wrapped = (("tf", hh), "zf") if t else (("kf", 9 + hh), "zk")
             ends = T[wrapped][:, C * hh + 15:C * hh + C:16]
-            if k == 0: scan(part(wrapped, hh), part(*src), ["%s%d" % src], ["zf" + s])
-            if k == 4: ts(part("zi", hh, 18), ends, T["scol"][:, :], 0.25, A.mult, A.add, ["zf" + s, "scol"], ["zi" + s])
+            if k == 0: scan(wrapped, hh, *src, q)
+            if k == 4: ts(part("zi", hh, 18), ends, T["scol"][:, :], 0.25, A.mult, A.add, reg(wrapped, hh) + ["scol"], ["zi" + s])
             if k == 5: ts(part("zb", hh, 18), part("zi", hh, 18), 1, 1, A.logical_shift_right, A.bitwise_and, ["zi" + s], ["zb" + s])
-            if k == 1: tt(part("fm", hh, 18), ends if t else part("zb", hh, 18), part("df", hh, 18), A.mult, [("zf" if t else "zb") + s, "df"], ["fm" + s])
+            if k == 1: tt(part("fm", hh, 18), ends if t else part("zb", hh, 18), part("df", hh, 18), A.mult, (reg(wrapped, hh) if t else ["zb" + s]) + ["df"], ["fm" + s])
             if k == 2: tt(part("af%d" % n, hh, 18), part("fm", hh, 18), part("af%d" % t, hh, 18), A.add, ["fm" + s, af % (t, hh)], [af % (n, hh)])
             if k == 3:
                 copy("v", off(n, hh), part("af%d" % n, hh, 18), [af % (n, hh)], [nxt + s])
@@ -366,11 +375,12 @@ def rank_program(g, core, T, topo):
             arrived(["list gone"], ("sz", sent["sz"]))
             for k in range(8): store("y", T.fo[k:k + 1, :], T["fr"][16 * k:16 * k + 1, :], ["fr", "list gone"])
         return {"j": j, "m": m, "c": c, "w": w, "o": o, "d": d, "l": l, "a": a, "x": x, "q": q_, "f": f, "h": h, "t": tf,
-                "k": lambda k, q: take(0, k), "p": lambda k, q: take(1, k), "g": g_, "y": y, "z": z, "i": i_, "r": r, "e": e_,
-                "P": lambda k, q: take(1, k), "u": u, "H": hp, "T": tp, "v": v_, "s": s_}
+                "k": lambda k, q: take(0, k, q), "p": lambda k, q: take(1, k, q), "g": g_, "y": y, "z": z, "i": i_, "r": r, "e": e_,
+                "P": lambda k, q: take(1, k, q), "u": u, "H": hp, "T": tp, "v": v_, "s": s_}
 
     def run(t, order):
-        for s in order.split(): steps(t - (s[0] in "pgyzir"))[s[0]](int(s[1]), s[2:])
+        for s in order.split():
+            for q in ([s[2:-1] + "0", s[2:-1] + "1"] if s[-1] == "*" else [s[2:]]): steps(t - (s[0] in "pgyzir"))[s[0]](int(s[1]), q)
 
     for b in range(4): ts(T["et"][:, 512 * b + b:512 * b + 512:4], iot[:, 0:128], T["p1"][:, :], 32.0, A.is_equal, A.mult, ["iot", "p1", "et"], ["et%d" % b])
     ts(T["uof"][:, :], iot[:, 0:8], 16.0, None, A.mult, None, ["iot"], ["uof"])
@@ -380,8 +390,8 @@ def rank_program(g, core, T, topo):
     copy("v", T["urq"][:, :].bitcast(dt.uint32), T["uq"][:, :].bitcast(dt.uint32).indirect(T["uof"][:, :]), ["u", "uof"], ["urq"])
     copy("s", T["urp"][:, :], T["up"][:, :].indirect(T["uof"][:, :]), ["u", "uof"], ["urp"])
     run(0, "q0 f0 h0s h1s h2s h3s")
-    copy("v", T["iw"][:, :].indirect(off(0, 0)), ci[:, :], ["ci", "aw0.0"], ["iw"])
-    scan(part("zj", 0), T["iw"][:, :], ["iw"], ["zj0"])
+    copy("v", T["iw"][:, :].indirect(off(0, 0)), ci[:, :], ["ci", "aw0.0"], ["iw"] + reg("iw", 0))
+    scan("zj", 0, "iw", 0)
     rounded(off(0, 1), 0, ["aw0.1"])
     copy("v", T["ivi"][:, :], off(0, 1), ["aw0.1"], ["ivi"])
     send(["ivi"], (hb, T["hiv"][:, 0:9], T["ivi"][:, 0:9], "hiv", rest[:8]), (hc, T["hiv"][:, 9:18], T["ivi"][:, 9:18], "hiv", rest[8:]), left="sod")

from concourse.bass import DstId, RemoteDMATransfer
from concourse.mybir import dt, AluOpType, ActivationFunctionType

C = 288
STEP = [4, 1, 2]
RAD = [2, 2, 2, 2, 2, 3, 3]
F32, BF, I32, U16, U8, MX = "float32", "bfloat16", "int32", "uint16", "uint8", "float8_e4m3fn_x4"

FIRST = ("j0* f1 c0s w0* o0* j1* m1* c1s* w1* o1* j2* m2* c2s* w2* o2* j3* m3* c3s* w3* o3* j4* m4* c4s* w4* o4* j5* m5* c5s* w5* o5* "
         "j6* m6* j7* m7* c7s* w6* o6* m8* d0 m9* d1 t1 k0* k4 k5 P0 k1 P4 k2 P5 k3 P1")
MEANS0 = "g0v g1s p2 y1 p3 y0 g3s g2s y3 i0 z0s y2 z1v z3v z2s "
MEANS1 = "p0 g0v g1s p1 y1 p2 y0 g3s g2s p3 y3 z0s i0 y2 z1v z3v z2s "
LATER = ("j0* r0 w0* o0* j1* m1* c1s* w1* o1* j2* m2* c2s* w2* o2* l0 j3* m3* c3s* w3* o3* d0 j4* m4* c4s* w4* o4* j5* m5* "
         "a0 c5s w5 a1 o5 a2 a3 x0s j6 m6 x3v x1s j70 x2s j71 m7 c7s* w60 q0 w61 o6* m8* f0 h0s f1 d1 m9* w7* o7* "
         "h1s h2s h3s t0v* k0* k1 k2 k3 t1")
LAST = ("p0 g0s p1 g1s p2 g2s p3 g3v u0 H0v T0s H1v T1s H2v T2s H3v T3s "
        "y0 y1 y2 y3 z0s z1s z2s z3v0 z3s1 r0 e0 "
        "l0 a0 a1 a2 a3 x0s0 x1s0 x2s0 x3v0 q0 x0s1 x1s1 x3v1 x2s1 q1 v0s v1v s0y s1y s2y s3y")
RUNS = ((0, 160), (160, C))


def _scratch():
    s = {}

    def sb(dtype, **names):
        for k in names: s[k] = ("sbuf", [128, names[k]], dtype)
    sb(I32, odi=18, b0=36, ivi=18, hiv=18, zi=36, zb=36, pidx=1, p15=1)
    for k in ("odd", "hod"): s[k] = ("dram", [128, 18], I32)
    sb(U16, ofc=18, uof=8, bu=18, lo=18 * 8, b1=36, b2=36, b3=18, hw3=18)
    for k in range(4): sb(U16, **{"aw%d" % k: 36})
    for k in (1, 2): sb(U16, **{a + "%d" % k: 18 for a in ("hw", "hx")})
    sb(BF, xin=4 * C, uin=512, vin=512, et=2048, zt=4 * C, xt=4 * C)
    sb(BF, ci=C, scc=C, jj=8 * C, kk=10 * C, cc=8 * C, zj=2 * C, fl=C, flp=C, tf=2 * C, zf=2 * C, iw=C)
    sb(F32, kf=11 * C, cf=8 * C, i4=C, zk=2 * C)
    sb(F32, iot=C, p1=1, p16=1, sct=1, scol=1, ne=16, nx=16, t1=16, sc16=16)
    sb(F32, gs=4 * C, bf=36, df=36, fm=36, af0=36, af1=36, af2=36, af3=36)
    sb(F32, fs=4 * C, ys=4 * C, rr=4 * C, fp=4 * C, fq=4 * C, yo=C, fr=C)
    for k, n in (("w", 512), ("e", 512), ("u", 128), ("ur", 128), ("v", 128)): sb(MX, **{k + "q": n}); sb(U8, **{k + "p": n})
    for k in range(4): sb(MX, **{"xq%d" % k: C}); sb(U8, **{"xs%d" % k: C})
    for k in range(3):
        for a in "zhr": sb(MX, **{"%sq%d" % (a, k): C}); sb(U8, **{"%ss%d" % (a, k): C})
    s["pd"] = ("psum", [128, 2048], F32)
    s["pr"] = ("psum", [128, 2048], F32)
    return s


SCRATCH = _scratch()
SEMAPHORES = ["cv", "cs", "ct", "cg", "lod", "lodd", "lx", "lu", "lv", "lwc", "lws", "store", "sent", "sod", "sz",
              "hod", "hiv", "hw1", "hw2", "hw3", "rw3", "hx1", "hx2", "rx1", "rx2", "hq0", "hq1", "hq2", "hs0", "hs1", "hs2",
              "roda", "rivb", "rivc", "rw1", "rw2", "rqa0", "rqa1", "rqa2", "rqb0", "rqb1", "rqb2", "rs0", "rs1", "rs2"]


def _mask(es):
    return sum(1 << e for e in es)


def _helpers(rc, dest, topo):
    h = [c for c in topo.cores_of(rc) if c != rc and topo.may_write(c, dest)]
    near = [c for c in h if topo.die(c) == topo.die(rc)]
    far = [c for c in h if topo.die(c) != topo.die(rc)]
    return near[0], far[0], near[1]


def _relay(g, core, rc, T, topo):
    rank, n = T.rank_of(rc), 0

    def fwd(dest, dst, src, sem):
        rid, pid = topo.addr(dest, core)
        g.remote_dma(out_ap=dst, in_ap=src, remote_sem=T.sem[sem], local_sem=T.sem["sent"], pid=pid, routing_id=rid, dma_engine_mask=topo.mask(core, dest))
        return len(topo.engines(core, dest))

    def on_chip(k):
        return len(topo.engines(rc, core)) // k
    dests = [T.cores[rank ^ s] for s in STEP]
    for t, dest in enumerate(dests):
        a, b, c = _helpers(rc, dest, topo)
        if t == 0:
            if core == a:
                g.wait_ge(T.sem["hod"], on_chip(4))
                n += fwd(dest, T["b0"][:, 0:18], T["hod"][:, :], "roda")
            for h, lo, sem, k in ((b, 0, "rivb", 2), (c, 9, "rivc", 4)):
                if core == h:
                    g.wait_ge(T.sem["hiv"], on_chip(k))
                    n += fwd(dest, T["b0"][:, 18 + lo:27 + lo], T["hiv"][:, lo:lo + 9], sem)
        for m, h, lo in (("w", 0, 0), ("x", 2, 18)):
            if t < 2 and core == _helpers(rc, dests[t + 1], topo)[h]:
                k = "%s%d" % (m, t + 1)
                g.wait_ge(T.sem["h" + k], on_chip(1))
                n += fwd(dests[t + 1], T["b%d" % (t + 1)][:, lo:lo + 18], T["h" + k][:, :], "r" + k)
        for h, lo, sem in ((a, 0, "rqa"), (b, C // 2, "rqb")):
            if core == h:
                k = "q%d" % t
                g.wait_ge(T.sem["h" + k], on_chip(2))
                n += fwd(dest, T["r" + k][:, lo:lo + C // 2].bitcast(dt.uint8), T["h" + k][:, lo:lo + C // 2].bitcast(dt.uint8), "%s%d" % (sem, t))
        if core == c:
            k = "s%d" % t
            g.wait_ge(T.sem["h" + k], on_chip(1))
            n += fwd(dest, T["r" + k][:, :], T["h" + k][:, :], "r" + k)
            if t == 2:
                g.wait_ge(T.sem["hw3"], on_chip(1))
                n += fwd(dest, T["b3"][:, :], T["hw3"][:, :], "rw3")
    if n: g.wait_ge(T.sem["sent"], n)


def rank_program(g, core, T, topo):
    rank = T.rank_of(core)
    if rank is None:
        for c in topo.cores_of(core):
            if T.rank_of(c) is not None: _relay(g, core, c, T, topo)
        return
    A = AluOpType
    COPY, RELU, SIGN = ActivationFunctionType.Copy, ActivationFunctionType.Relu, ActivationFunctionType.Sign
    eng = {"v": g.vector, "s": g.scalar, "t": g.tensor, "y": g.sync, "g": g}
    count, last_write, readers = {}, {}, {}
    known = {q: {} for q in eng}

    def settle(q, events):
        best = {}
        for s, n, snap in events:
            if known[q].get(s, 0) < n and (s not in best or best[s][0] < n): best[s] = (n, snap)
        for s in list(best):
            if any(o != s and best[o][1].get(s, 0) >= best[s][0] for o in best): del best[s]
        for s in best:
            n, snap = best[s]
            eng[q].wait_ge(T.sem[s], n)
            for k, m in list(snap.items()) + [(s, n)]: known[q][k] = max(known[q].get(k, 0), m)

    def call(q, make, reads, writes, sem=None, step=1):
        banks = [r for r in reads if r[:2] in ("pd", "pr")]
        events = []
        for r in reads: events += last_write.get(r, [])
        for r in writes + banks: events += last_write.get(r, []) + readers.get(r, [])
        settle(q, events)
        ins = make(eng[q])
        s = sem or "c" + q
        count[s] = count.get(s, 0) + step
        ins.then_inc(T.sem[s], step)
        e = (s, count[s], dict(known[q]))
        for r in reads: readers.setdefault(r, []).append(e)
        for r in writes: last_write[r], readers[r] = [e], []

    def arrived(regions, *events):
        for r in regions: last_write[r], readers[r] = [(s, n, {}) for s, n in events], []

    def load(q, dst, src, sem, writes, after=()): call(q, lambda e: e.dma_start(dst, src), list(after), writes, sem, 16)

    def store(q, dst, src, reads): call(q, lambda e: e.dma_start(dst, src), reads, [], "store", 16)

    def tt(out, in0, in1, op, reads, writes): call("v", lambda e: e.tensor_tensor(out, in0, in1, op), reads, writes)

    def ts(out, in0, s1, s2, op0, op1, reads, writes):
        if op1 is None: call("v", lambda e: e.tensor_scalar(out, in0, s1, None, op0), reads, writes)
        else: call("v", lambda e: e.tensor_scalar(out, in0, s1, s2, op0, op1), reads, writes)

    def copy(q, out, in_, reads, writes, scale=1.0):
        if q == "s" and scale == 1.0: call("s", lambda e: e.activation(out, in_, COPY), reads, writes)
        elif q == "s": call("s", lambda e: e.activation(out, in_, COPY, scale=scale), reads, writes)
        elif scale == 1.0: call("v", lambda e: e.tensor_copy(out, in_), reads, writes)
        else: ts(out, in_, scale, None, A.mult, None, reads, writes)

    def quant(q, s, in_, reads, writes): call("v", lambda e: e.quantize_mx(q, s, in_), reads, writes)

    def mm(out, lq, ls, rq, rs, reads, writes): call("t", lambda e: e.matmul_mx(out, lq, ls, rq, rs, True, True), reads, writes)

    sent = {"sent": 0, "sod": 0, "sz": 0}
    dests = [T.cores[rank ^ s] for s in STEP]
    back = [[len(topo.engines(h, core)) for h in _helpers(d, core, topo)] for d in dests]

    def send(reads, *parts, left="sent"):
        settle("g", [e for r in reads for e in last_write.get(r, [])])
        if len(parts) == 1:
            h, dst, src, sem, es = parts[0]
            rid, pid = topo.addr(h, core)
            g.remote_dma(out_ap=dst, in_ap=src, remote_sem=T.sem[sem], local_sem=T.sem[left], pid=pid, routing_id=rid, dma_engine_mask=_mask(es))
        else:
            moves = []
            for h, dst, src, sem, es in parts:
                rid, pid = topo.addr(h, core)
                moves.append(RemoteDMATransfer(dst_ids=[DstId(rid=rid, pnc=pid)], dma_engine_mask=_mask(es), remote_sem=T.sem[sem], src=src, dst=dst))
            g.remote_dma_fused(moves, local_sem=T.sem[left])
        sent[left] += sum(len(p[4]) for p in parts)

    load("y", T["odd"][:, :], T.od[:, :], "lodd", ["odd"])
    load("y", T["odi"][:, :], T.od[:, :], "lod", ["odi"])
    load("y", T["uin"][:, :], T.u[:, :], "lu", ["uin"])
    load("y", T["xin"][:, :], T.x[:, :], "lx", ["xin"])
    ha, hb, hc = _helpers(core, dests[0], topo)
    es = topo.engines(core, ha)
    rest = [e for e in es if e not in es[1::4]]
    iot, ci = T["iot"], T["ci"]
    call("v", lambda e: e.memset(T["et"][:, :], 0.0), [], ["et"])
    call("g", lambda e: e.iota(T["pidx"][:, :], [[1, 1]], 0, 1), [], ["pidx"])
    call("g", lambda e: e.iota(iot[:, :], [[1, C]], 0, 0, allow_small_or_imprecise_dtypes=True), [], ["iot"])
    send(["odd"], (ha, T["hod"][:, :], T["odd"][:, :], "hod", es[1::4]), left="sod")
    call("g", lambda e: e.iota(T["i4"][:, :], [[4, C]], 1, 0, allow_small_or_imprecise_dtypes=True), [], ["i4"])
    arrived(["b0.o"], ("roda", back[0][0]))
    arrived(["b0.i"], ("rivb", back[0][1]), ("rivc", back[0][2]))
    arrived(["b3.o"], ("rw3", back[2][2]))
    for t in range(3):
        if t:
            arrived(["b%d.o" % t], ("rw%d" % t, back[t][0]))
            arrived(["b%d.i" % t], ("rx%d" % t, back[t][2]))
        arrived(["rz%d" % t], ("rqa%d" % t, back[t][0]), ("rqb%d" % t, back[t][1]), ("rs%d" % t, back[t][2]))

    ts(T["p15"][:, :], T["pidx"][:, :], 15, None, A.bitwise_and, None, ["pidx"], ["p15"])
    copy("v", T["p1"][:, :], T["pidx"][:, :], ["pidx"], ["p1"])
    copy("v", T["p16"][:, :], T["p15"][:, :], ["p15"], ["p16"])
    ts(T["nx"][:, :], iot[:, 0:16], T["p16"][:, :], 1.0, A.subtract, A.is_equal, ["iot", "p16"], ["nx"])
    ts(T["ne"][:, :], iot[:, 0:16], T["p16"][:, :], None, A.not_equal, None, ["iot", "p16"], ["ne"])
    ts(T["t1"][:, :], T["nx"][:, :], 1048575.0, None, A.mult, None, ["nx"], ["t1"])
    ts(T["ofc"][:, :], iot[:, 0:18], 0.0, T["p16"][:, :], A.mult, A.add, ["iot", "p16"], ["ofc"])
    tt(T["sc16"][:, :], T["t1"][:, :], T["ne"][:, :], A.add, ["t1", "ne"], ["sc16"])
    ts(T["sct"][:, :], T["p16"][:, :], 15.0, 1.0 - 2.0 ** -20, A.is_equal, A.mult, ["p16"], ["sct"])
    ts(ci[:, :], iot[:, :], -144.0, None, A.add, None, ["iot"], ["ci"])
    ts(T["scol"][:, :], T["sct"][:, :], 2.0 ** -20, None, A.add, None, ["sct"], ["scol"])
    copy("s", T["scc"][:, :], T["sc16"][:, :].indirect(T["ofc"][:, :]), ["sc16", "ofc"], ["scc"])

    def part(name, b, n=C): return T[name][:, n * b:n * b + n]

    def bank(p, b, n=C): return T[p][:, 512 * b:512 * b + n]

    def off(t, h): return part("aw%d" % t, h, 18)

    def runs(q):
        ks = [int(q[-1])] if q[-1:].isdigit() else [0, 1]
        return ks, RUNS[ks[0]][0], RUNS[ks[-1]][1]

    def cols(name, k, q): return T[name][:, C * k + runs(q)[1]:C * k + runs(q)[2]]

    def offs(name, first, q): return T[name][:, first + runs(q)[1] // 16:first + runs(q)[2] // 16]

    def reg(name, k, q=""): return ["%s%d.%d" % (name, k, r) for r in runs(q)[0]]

    def scan(out, ko, src, k, q=""):
        call("v", lambda e: e.tensor_tensor_scan(cols(out, ko, q), cols("scc", 0, q), cols(src, k, q), 0.0, A.mult, A.add), ["scc"] + reg(src, k, q), reg(out, ko, q))

    def rounded(out, z, writes, q=""):
        ts(out, T["zj"][:, C * z + runs(q)[1] + 15:C * z + runs(q)[2]:16], T["scol"][:, :], 144.25, A.mult, A.add, reg("zj", z, q) + ["scol"], writes)

    def whole(tile): return [r for b in range(4) for r in reg(tile, b)]

    def state(n):
        q, s = T["xq%d" % n], T["xs%d" % n]
        if n: quant(q[:, :], s[:, :], T["xt"][:, :], whole("xt"), ["x%d" % n])
        else: quant(q[:, :], s[:, :], T["xin"][:, :], ["xin"], ["x0"])
        mm(bank("pr", 0), T["urq"][:, :], T["urp"][:, :], q[:, :], s[:, :], ["urq", "urp", "x%d" % n], ["pr0"])
        for b in range(4): mm(bank("pd", b), part("eq", b, 128), part("ep", b, 128), q[:, :], s[:, :], ["e", "x%d" % n], ["pd%d" % b])

    stage, base, wsrc = [None], [None], [0]
    for i, r in enumerate(RAD):
        first = len(stage) - 1
        for m in range(r - 1): stage.append(i); base.append(first)
        wsrc.append(len(stage) - 1)

    def steps(t):
        n, p = t + 1, t - 1
        own, nxt = "aw%d." % t, "aw%d." % n

        kk, cc = ("kk", "cc") if t else ("kf", "cf")

        def j(k, q):
            if k: return copy("s", cols("jj", k, q), part("jj", k - 1).indirect(offs("lo", 18 * stage[k], q)), reg("jj", k - 1) + reg("lo", stage[k], q), reg("jj", k, q))
            if t: return copy("s", cols("jj", 0, q), T["iw"][:, :].indirect(offs("b%d" % t, 0, q)), ["iw", "b%d.o" % t], reg("jj", 0, q))
            if 0 in runs(q)[0]: copy("v", T["bu"][:, :], T["b0"][:, 0:18], ["b0.o"], ["bu"])
            copy("s", cols("jj", 0, q), T["iw"][:, :].indirect(offs("bu", 0, q)), ["iw", "bu"], reg("jj", 0, q))

        def m(k, q):
            if k == 1 and t: return tt(cols(kk, 1, q), cols("jj", 0, q), cols("ci", 0, q), A.min, reg("jj", 0, q) + ["ci"], reg(kk, 1, q))
            other = (cc if base[k] == k - 1 else kk, base[k])
            tt(cols(kk, k, q), part(kk, k - 1).indirect(offs("lo", 18 * stage[k], q)), cols(*other, q), A.min,
               reg(kk, k - 1) + reg("lo", stage[k], q) + reg(*other, q), reg(kk, k, q))

        def c(k, q): copy(q[0], cols(cc, k, q), cols(kk, k, q), reg(kk, k, q), reg(cc, k, q))

        def w(i, q):
            src = "kk" if i == len(RAD) else "jj"
            scan("zj", i % 2, src, wsrc[i], q)

        def o(i, q): rounded(offs("lo", 18 * i, q), i % 2, reg("lo", i, q), q)

        def d(k, q):
            if k == 0: ts(T["bf"][:, :], T["b%d" % t][:, :], 0.25, None, A.add, None, ["b%d.o" % t, "b%d.i" % t], ["bf"])
            else: tt(T["df"][:, :], T["bf"][:, :], T["af%d" % t][:, :], A.subtract, ["bf", "af%d.0" % t, "af%d.1" % t], ["df"])

        zq, zs, zr, lb = ("zq2", "zs2", "z2", "pd") if t == 3 else ("rq%d" % p, "rs%d" % p, "rz%d" % p, "pr")

        def l(k, q):
            for b in range(4): mm(bank(lb, b), part("wq", b, 128), part("wp", b, 128), T[zq][:, :], T[zs][:, :], ["wq", "wp", zr], [lb + str(b)])

        def a(b, q): tt(part("rr", b), bank(lb, b), part("gs", b), A.add, [lb + str(b), "gs%d" % b], ["rr%d" % b])

        def moved(q, tile, b, src, offsets, first, region, scale):
            ks, c0, c1 = runs(q)
            copy(q[0], T[tile][:, 4 * c0 + b:4 * c1:4], part(src, b).indirect(offs(offsets, first, q)), [src + str(b), region], reg(tile, b, q), scale)

        def x(b, q): moved(q, "xt", b, "rr", "aw%d" % t, 18, own + "1", 2.0 ** -5)

        def f(k, q):
            if k == 0: call("s", lambda e: e.activation(T["fl"][:, :], bank("pr", 0), SIGN), ["pr0"], ["fl"])
            elif t == 0: tt(part("kf", 0), T["fl"][:, :].indirect(off(0, 0)), T["i4"][:, :], A.add, ["fl", "aw0.0", "i4"], reg("kf", 0))
            else: call("s", lambda e: e.activation(T["flp"][:, :], T["fl"][:, :].indirect(off(t, 0)), RELU, scale=T["scol"][:, :]), ["fl", own + "0", "scol"], ["flp"])

        def h(b, q): copy(q, part("fs", b), bank("pd", b), ["pd%d" % b], ["fs%d" % b])

        def tf(k, q):
            if t == 0: copy("s", part("kf", 10), part("kf", 9).indirect(off(0, 1)), reg("kf", 9) + ["aw0.1"], reg("kf", 10))
            elif k == 0: copy(q[0], cols("tf", 0, q), T["flp"][:, :].indirect(offs("lo", 18 * len(RAD), q)), ["flp"] + reg("lo", len(RAD), q), reg("tf", 0, q))
            else: copy("s", part("tf", 1), part("tf", 0).indirect(off(t, 1)), reg("tf", 0) + [own + "1"], reg("tf", 1))

        def take(hh, k, q):
            s, af = str(hh), "af%d.%d"
            src, wrapped = (("tf", hh), "zf") if t else (("kf", 9 + hh), "zk")
            ends = T[wrapped][:, C * hh + 15:C * hh + C:16]
            if k == 0: scan(wrapped, hh, *src, q)
            if k == 4: ts(part("zi", hh, 18), ends, T["scol"][:, :], 0.25, A.mult, A.add, reg(wrapped, hh) + ["scol"], ["zi" + s])
            if k == 5: ts(part("zb", hh, 18), part("zi", hh, 18), 1, 1, A.logical_shift_right, A.bitwise_and, ["zi" + s], ["zb" + s])
            if k == 1: tt(part("fm", hh, 18), ends if t else part("zb", hh, 18), part("df", hh, 18), A.mult, (reg(wrapped, hh) if t else ["zb" + s]) + ["df"], ["fm" + s])
            if k == 2: tt(part("af%d" % n, hh, 18), part("fm", hh, 18), part("af%d" % t, hh, 18), A.add, ["fm" + s, af % (t, hh)], [af % (n, hh)])
            if k == 3:
                copy("v", off(n, hh), part("af%d" % n, hh, 18), [af % (n, hh)], [nxt + s])
                name = "h%s%d" % ("wx"[hh], n)
                if n < 3: send([nxt + s], (_helpers(core, dests[n], topo)[2 * hh], T[name][:, :], off(n, hh), name, es))
                elif hh == 0: send([nxt + s], (_helpers(core, dests[t], topo)[2], T[name][:, :], off(n, hh), name, es), left="sz")

        def g_(b, q): copy(q, part("gs", b), part("fs", b).indirect(off(n, 0)), ["fs%d" % b, nxt + "0"], ["gs%d" % b])

        zo, ro = ("b3", "b3.o") if n >= 3 else ("aw%d" % n, nxt + "0")

        def u(k, q):
            for b in range(4): mm(bank("pr", b), part("eq", b, 128), part("ep", b, 128), T["rq2"][:, :], T["rs2"][:, :], ["e", "rz2"], ["pr%d" % b])

        def hp(b, q): copy(q, part("fp", b), bank("pr", b), ["pr%d" % b], ["fp%d" % b])

        def tp(b, q): copy(q, part("fq", b), part("fp", b), ["fp%d" % b], ["fq%d" % b])

        def y(b, q):
            if n < 3: tt(part("ys", b), part("gs", b), bank("pd", b), A.add, ["gs%d" % b, "pd%d" % b], ["ys%d" % b])
            else: tt(part("ys", b), part("fp", b).indirect(T[zo][:, :]), part("fq", b), A.add, ["fp%d" % b, "fq%d" % b, ro], ["ys%d" % b])

        def z(b, q): moved(q, "zt", b, "ys", zo, 0, ro, 2.0 ** -6)

        def i_(k, q): copy("s", T["iw"][:, :], ci[:, :].indirect(off(n, 1)), ["ci", nxt + "1"], ["iw"])

        def codes(q, s, region):
            hq, half = T["hq%d" % t], C // 2
            ha, hb, hc = _helpers(core, dests[t], topo)
            send([region], (ha, hq[:, 0:half].bitcast(dt.uint8), q[:, 0:half].bitcast(dt.uint8), "hq%d" % t, es[1::2]),
                 (hb, hq[:, half:C].bitcast(dt.uint8), q[:, half:C].bitcast(dt.uint8), "hq%d" % t, es[0::2]))
            send([region], (hc, T["hs%d" % t][:, :], s[:, :], "hs%d" % t, es))

        def r(k, q):
            quant(T["zq%d" % t][:, :], T["zs%d" % t][:, :], T["zt"][:, :], whole("zt"), ["z%d" % t])
            if n < 3: codes(T["zq%d" % t], T["zs%d" % t], "z%d" % t)

        def q_(k, q):
            if t < 3: state(t)
            if t == 2: codes(T["xq2"], T["xs2"], "x2")
            if t == 3:
                c0, c1 = RUNS[k]
                r = "x3.%d" % k
                quant(T["xq3"][:, c0:c1], T["xs3"][:, c0:c1], T["xt"][:, 4 * c0:4 * c1], ["xt%d.%d" % (b, k) for b in range(4)], [r])
                mm(bank("pr", k, c1 - c0), T["vq"][:, :], T["vp"][:, :], T["xq3"][:, c0:c1], T["xs3"][:, c0:c1], ["v", r], ["pr%d" % k])
                store("y", T.oc[:, 4 * c0:4 * c1], T["xq3"][:, c0:c1].bitcast(dt.uint8), [r])

        def v_(k, q):
            c0, c1 = RUNS[k]
            copy(q, T["yo"][:, c0:c1], bank("pr", k, c1 - c0), ["pr%d" % k], ["yo%d" % k])
            if k: store("s", T.y[:, :], T["yo"][:, :], ["yo0", "yo1"])

        def s_(m, q): store(q, T.osc[4 * m:4 * m + 4, :], T["xs3"][32 * m:32 * m + 4, :], ["x3.0", "x3.1"])

        def e_(k, q):
            quant(T["vq"][:, :], T["vp"][:, :], T["vin"][:, :], ["vin"], ["v"])
            copy("s", T["fr"][:, :], iot[:, :].indirect(off(3, 0)), ["iot", "aw3.0"], ["fr"])
            arrived(["list gone"], ("sz", sent["sz"]))
            for k in range(8): store("y", T.fo[k:k + 1, :], T["fr"][16 * k:16 * k + 1, :], ["fr", "list gone"])
        return {"j": j, "m": m, "c": c, "w": w, "o": o, "d": d, "l": l, "a": a, "x": x, "q": q_, "f": f, "h": h, "t": tf,
                "k": lambda k, q: take(0, k, q), "p": lambda k, q: take(1, k, q), "g": g_, "y": y, "z": z, "i": i_, "r": r, "e": e_,
                "P": lambda k, q: take(1, k, q), "u": u, "H": hp, "T": tp, "v": v_, "s": s_}

    def run(t, order):
        for s in order.split():
            for q in ([s[2:-1] + "0", s[2:-1] + "1"] if s[-1] == "*" else [s[2:]]): steps(t - (s[0] in "pgyzir"))[s[0]](int(s[1]), q)

    for b in range(4): ts(T["et"][:, 512 * b + b:512 * b + 512:4], iot[:, 0:128], T["p1"][:, :], 32.0, A.is_equal, A.mult, ["iot", "p1", "et"], ["et%d" % b])
    ts(T["uof"][:, :], iot[:, 0:8], 16.0, None, A.mult, None, ["iot"], ["uof"])
    copy("v", off(0, 0), T["odi"][:, :], ["odi"], ["aw0.0"])
    quant(T["uq"][:, :], T["up"][:, :], T["uin"][:, :], ["uin"], ["u"])
    quant(T["eq"][:, :], T["ep"][:, :], T["et"][:, :], ["et0", "et1", "et2", "et3"], ["e"])
    copy("v", T["urq"][:, :].bitcast(dt.uint32), T["uq"][:, :].bitcast(dt.uint32).indirect(T["uof"][:, :]), ["u", "uof"], ["urq"])
    copy("s", T["urp"][:, :], T["up"][:, :].indirect(T["uof"][:, :]), ["u", "uof"], ["urp"])
    run(0, "q0 f0 h0s h1s h2s h3s")
    copy("v", T["iw"][:, :].indirect(off(0, 0)), ci[:, :], ["ci", "aw0.0"], ["iw"] + reg("iw", 0))
    scan("zj", 0, "iw", 0)
    rounded(off(0, 1), 0, ["aw0.1"])
    copy("v", T["ivi"][:, :], off(0, 1), ["aw0.1"], ["ivi"])
    send(["ivi"], (hb, T["hiv"][:, 0:9], T["ivi"][:, 0:9], "hiv", rest[:8]), (hc, T["hiv"][:, 9:18], T["ivi"][:, 9:18], "hiv", rest[8:]), left="sod")
    arrived(["lists gone"], ("sod", sent["sod"]))
    load("y", T["wq"][:, :].bitcast(dt.uint8), T.wc[:, :], "lwc", ["wq"], ["lists gone"])
    load("y", T["wp"][:, :], T.ws[:, :], "lws", ["wp"])
    load("y", T["vin"][:, :], T.v[:, :], "lv", ["vin"])
    ts(T["af0"][:, :], T["aw0"][:, :], 0.25, None, A.add, None, ["aw0.0", "aw0.1"], ["af0.0", "af0.1"])
    for t, order in enumerate((FIRST, MEANS0 + LATER, MEANS1 + LATER, LAST)): run(t, order)
    for s in ("cv", "cs", "ct", "cg", "store"): g.wait_ge(T.sem[s], count[s])
    for s in sent: g.wait_ge(T.sem[s], sent[s])
